import numpy as np
CORES = [33,38,57,62,81,86,161,166,185,190,209,214]
N = 12
TK = 512
D = 128 * N
EPS = 0.01
def setup_inputs(rng):
    return {"x": (rng.standard_normal((N, 128, TK), dtype=np.float32) * (0.5 + np.abs(rng.standard_normal((1, 1, TK), dtype=np.float32))) + rng.standard_normal((1, 1, TK), dtype=np.float32)), "w": (rng.standard_normal((N, 128, 128), dtype=np.float32) / 11)}
def setup_inputs_big(rng):
    d = setup_inputs(rng)
    for k in ("x", "w"): d[k] = (d[k].astype(np.float32) * 1048576.0).astype(d[k].dtype)
    return d
def setup_inputs_small(rng):
    d = setup_inputs(rng)
    for k in ("x", "w"): d[k] = (d[k].astype(np.float32) * (1 / 1048576.0)).astype(d[k].dtype)
    return d
def setup_inputs_apart(rng):
    d = setup_inputs(rng)
    f = (10.0 ** rng.permutation(np.linspace(-1.5, 1.5, N))).astype(np.float32).reshape(N, 1, 1)
    for k in ("x", "w"): d[k] = (d[k].astype(np.float32) * f).astype(d[k].dtype)
    return d
def setup_inputs_mixed(rng):
    d = setup_inputs(rng)
    f = (10.0 ** rng.uniform(-3, 3, (1, 1, TK))).astype(np.float32); shape = rng.integers(3, size=(1, 1, TK))
    for k in ("x",):
        x = d[k].astype(np.float32)
        m = x.mean(axis=(0, 1), keepdims=True); level = m + np.sign(x - m) * np.abs(x - m).mean(axis=(0, 1), keepdims=True) * rng.uniform(0.9, 1.1, x.shape).astype(np.float32)
        other = x * np.where(rng.random(x.shape) < 0.5, 0.1, 1.0).astype(np.float32)
        d[k] = (np.where(shape == 1, level, np.where(shape == 2, other, x)) * f).astype(d[k].dtype)
    return d
def reference(x, w):
    X = x.astype(np.float64)
    Z = X
    Z = Z / np.sqrt((Z ** 2).sum(axis=(0, 1)) / D + EPS)
    s = sum(w[r].astype(np.float64).T @ Z[r] for r in range(N)).astype(np.float32)
    return {"y": np.broadcast_to(s, (N,) + s.shape)}

@@ -1,0 +1,203 @@
+from concourse.bass import DstId, RemoteDMATransfer
+from concourse.mybir import AluOpType, AxisListType, ActivationFunctionType
+
+WORLD = 256
+NR = 12
+D = 128 * NR
+EPS = 0.01
+NCH = 6
+BW = 43
+SW = 44
+HWD = NCH * SW
+STARTS = (0, 43, 85)
+
+F = "float32"
+SCRATCH = {
+    "xs": ("sbuf", [128, 512], F), "ws": ("sbuf", [128, 128], F), "x2": ("sbuf", [128, 512], F),
+    "one3": ("sbuf", [128, 4], F), "stg": ("sbuf", [128, 2 * HWD], F), "Y": ("sbuf", [128, 512], F),
+    "L": ("sbuf", [128, 2 * HWD], F), "C": ("sbuf", [128, HWD], F), "R": ("sbuf", [128, HWD], F),
+    "T1": ("sbuf", [128, 3 * SW], F), "T2": ("sbuf", [128, SW], F), "T3": ("sbuf", [128, SW], F),
+    "sst": ("sbuf", [128, 4], F), "sq": ("sbuf", [128, 4], F), "rs": ("sbuf", [128, 4], F),
+    "ones43": ("sbuf", [128, SW], F), "isel": ("sbuf", [128, SW], F), "ones128": ("sbuf", [128, 128], F),
+    "dg": ("sbuf", [128, SW], F), "O": ("sbuf", [128, SW], F),
+    "pc0": ("psum", [128, 512], F), "pc1": ("psum", [128, 512], F), "pc2": ("psum", [128, 512], F),
+    "pc3": ("psum", [128, 512], F), "ps0": ("psum", [128, 512], F), "ps1": ("psum", [128, 512], F),
+}
+SEMAPHORES = ["sw", "sx0", "sx1", "sm", "sq0", "sq1", "pm0", "pm1", "pm2", "pm3", "pss0", "pss1", "cp0", "cp1",
+              "arrL", "arrR", "arrY0", "arrY1", "lsem", "st0", "st1",
+              "si", "cs", "own", "s1", "s2", "s3", "s4", "s5", "s6", "t"]
+
+
+def _bits(m):
+    return [i for i in range(16) if (m >> i) & 1]
+
+
+def _mk(lst):
+    return sum(1 << i for i in lst)
+
+
+def _layout(T, topo):
+    ranks = list(T.cores)
+    key = lambda c: (topo.host(c), topo.chip(c))
+    chips = []
+    for c in ranks:
+        if key(c) not in chips:
+            chips.append(key(c))
+    dies = sorted(set(topo.die(c) for c in ranks))
+    ranks_of = [[c for c in ranks if key(c) == ch] for ch in chips]
+    agent = []
+    for ch in chips:
+        row = []
+        for d in dies:
+            cand = [c for c in range(WORLD) if key(c) == ch and topo.die(c) == d and c not in ranks
+                    and all(topo.may_write(c, r) for r in ranks)]
+            row.append(cand[0])
+        agent.append(row)
+    return ranks, chips, ranks_of, agent
+
+
+def _scatter_plan(k, h, agent, topo):
+    me = agent[k][h]
+    others = [(k + j) % NCH for j in range(1, NCH)]
+    others.sort(key=lambda b: 1 if topo.same_plane(me, agent[b][h]) else 0)
+    eng = _bits(topo.mask(me, agent[others[0]][h]))
+    for b in others:
+        eng = [e for e in eng if e in _bits(topo.mask(me, agent[b][h]))]
+    plan = [(b, eng[2 * j:2 * j + 2]) for j, b in enumerate(others[:4])]
+    plan.append((others[4], eng))
+    return plan
+
+
+def _rank(g, core, T, topo, ranks_of, agent, k):
+    S = T.sem
+    i = ranks_of[k].index(core)
+    Act = ActivationFunctionType
+    g.sync.dma_start(T.ws[:], T.w[:]).then_inc(S.sw, 16)
+    g.scalar.dma_start(T.xs[:, 0:256], T.x[:, 0:256]).then_inc(S.sx0, 16)
+    g.sync.dma_start(T.xs[:, 256:512], T.x[:, 256:512]).then_inc(S.sx1, 16)
+    g.vector.memset(T.one3[:], 1.0).then_inc(S.sm, 1)
+    for h in range(2):
+        g.scalar.wait_ge(S["sx%d" % h], 16)
+        g.scalar.activation(T.x2[:, 256 * h:256 * h + 256], T.xs[:, 256 * h:256 * h + 256], Act.Square).then_inc(S["sq%d" % h], 1)
+    g.tensor.wait_ge(S.sw, 16)
+    for h in range(2):
+        g.tensor.wait_ge(S["sx%d" % h], 16)
+        for c in (2 * h, 2 * h + 1):
+            g.tensor.matmul(T["pc%d" % c][:, 0:128], T.ws[:], T.xs[:, 128 * c:128 * c + 128], True, True).then_inc(S["pm%d" % c], 1)
+        if h == 0:
+            g.tensor.wait_ge(S.sm, 1)
+        g.tensor.wait_ge(S["sq%d" % h], 1)
+        for cc in range(2):
+            c = 2 * h + cc
+            g.tensor.matmul(T["ps%d" % h][:, 3 * cc:3 * cc + 3], T.x2[:, 128 * c:128 * c + 128], T.one3[:, 0:3], True, True).then_inc(S["pss%d" % h], 1)
+    for h in range(2):
+        cp = S["cp%d" % h]
+        c = 2 * h
+        g.vector.wait_ge(S["pm%d" % c], 1)
+        for j in range(3):
+            s = SW * (3 * c + j)
+            g.vector.tensor_copy(T.stg[:, s:s + BW], T["pc%d" % c][:, STARTS[j]:STARTS[j] + BW]).then_inc(cp, 1)
+        c = 2 * h + 1
+        g.scalar.wait_ge(S["pm%d" % c], 1)
+        for j in range(3):
+            s = SW * (3 * c + j)
+            g.scalar.activation(T.stg[:, s:s + BW], T["pc%d" % c][:, STARTS[j]:STARTS[j] + BW], Act.Copy).then_inc(cp, 1)
+        g.vector.wait_ge(S["pss%d" % h], 2)
+        g.vector.tensor_copy(T.stg[:, HWD * h + BW:HWD * h + HWD:SW], T["ps%d" % h][:, 0:6]).then_inc(cp, 1)
+    for h in range(2):
+        a = agent[k][h]
+        rid, pid = topo.addr(a, core)
+        m = _mk(_bits(topo.mask(core, a))[0:8])
+        g.wait_ge(S["cp%d" % h], 7)
+        g.remote_dma(T.L[:, HWD * i:HWD * i + HWD], T.stg[:, HWD * h:HWD * h + HWD], S.arrL, S.lsem, pid, rid, m)
+    need = 8 * (NCH - 1) + 2
+    g.sync.wait_ge(S.arrY0, need)
+    g.sync.dma_start(T.y[:, 0:256], T.Y[:, 0:256]).then_inc(S.st0, 16)
+    g.scalar.wait_ge(S.arrY1, need)
+    g.scalar.dma_start(T.y[:, 256:512], T.Y[:, 256:512]).then_inc(S.st1, 16)
+    g.wait_ge(S.lsem, 16)
+    g.wait_ge(S.st0, 16)
+    g.wait_ge(S.st1, 16)
+
+
+def _agent(g, core, T, topo, ranks, ranks_of, agent, k, h):
+    S = T.sem
+    A = AluOpType
+    start = STARTS[k % 3]
+    own = slice(SW * k, SW * k + SW)
+    g.vector.memset(T.ones43[:, 0:BW], 1.0).then_inc(S.sm, 1)
+    g.vector.memset(T.ones128[:], 1.0).then_inc(S.sm, 1)
+    g.wait_ge(S.sm, 2)
+    g.affine_select(T.isel[:, 0:BW], T.ones43[:, 0:BW], [[-1, BW]], A.is_equal, 0.0, -start, 1).then_inc(S.si, 1)
+    g.vector.wait_ge(S.arrL, 16)
+    g.vector.tensor_tensor(T.C[:], T.L[:, 0:HWD], T.L[:, HWD:2 * HWD], A.add).then_inc(S.cs, 1)
+    g.vector.tensor_tensor(T.R[:, own], T.L[:, own], T.L[:, HWD + SW * k:HWD + SW * k + SW], A.add).then_inc(S.own, 1)
+    plan = _scatter_plan(k, h, agent, topo)
+    g.wait_ge(S.cs, 1)
+    trs = []
+    for b, eng in plan[:4]:
+        rid, pid = topo.addr(agent[b][h], core)
+        trs.append(RemoteDMATransfer(dst_ids=[DstId(rid=rid, pnc=pid)], dma_engine_mask=_mk(eng), remote_sem=S.arrR,
+                                     srcs=[T.C[:, SW * b:SW * b + SW]], dsts=[T.R[:, own]], alu_op=0))
+    g.remote_dma_fused(trs, local_sem=S.lsem)
+    b, eng = plan[4]
+    rid, pid = topo.addr(agent[b][h], core)
+    g.remote_dma(T.R[:, own], T.C[:, SW * b:SW * b + SW], S.arrR, S.lsem, pid, rid, _mk(eng))
+    sent = sum(len(e) for _, e in plan)
+    need = 0
+    for kk in range(NCH):
+        if kk != k:
+            need += sum(len(e) for b2, e in _scatter_plan(kk, h, agent, topo) if b2 == k)
+    g.vector.wait_ge(S.arrR, need)
+    g.vector.wait_ge(S.own, 1)
+    g.vector.tensor_reduce(T.sst[:, 0:1], T.R[:, BW:HWD:SW], AxisListType.X, A.add).then_inc(S.s1, 1)
+    g.scalar.wait_ge(S.s1, 1)
+    g.scalar.activation(T.sq[:, 0:1], T.sst[:, 0:1], ActivationFunctionType.Sqrt, bias=EPS, scale=1.0 / D).then_inc(S.s2, 1)
+    g.vector.tensor_tensor(T.T1[:], T.R[:, 0:3 * SW], T.R[:, 3 * SW:6 * SW], A.add).then_inc(S.t, 1)
+    g.vector.wait_ge(S.t, 1)
+    g.vector.tensor_tensor(T.T2[:], T.T1[:, 0:SW], T.T1[:, SW:2 * SW], A.add).then_inc(S.t, 1)
+    g.vector.wait_ge(S.t, 2)
+    g.vector.tensor_tensor(T.T3[:], T.T2[:], T.T1[:, 2 * SW:3 * SW], A.add).then_inc(S.t, 1)
+    g.vector.wait_ge(S.s2, 1)
+    g.vector.reciprocal(T.rs[:, 0:1], T.sq[:, 0:1]).then_inc(S.s3, 1)
+    g.vector.wait_ge(S.s3, 1)
+    g.vector.wait_ge(S.si, 1)
+    g.vector.tensor_scalar(T.dg[:, 0:BW], T.isel[:, 0:BW], T.rs[:, 0:1], None, A.mult).then_inc(S.s4, 1)
+    g.tensor.wait_ge(S.sm, 2)
+    g.tensor.wait_ge(S.s4, 1)
+    g.tensor.matmul(T.pc0[:, 0:BW], T.ones128[:], T.dg[:, 0:BW], True, True).then_inc(S.s5, 1)
+    g.vector.wait_ge(S.s5, 1)
+    g.vector.wait_ge(S.t, 3)
+    g.vector.tensor_tensor(T.O[:, 0:BW], T.T3[:, 0:BW], T.pc0[:, 0:BW], A.mult).then_inc(S.s6, 1)
+    lo = 1 if k % 3 == 2 else 0
+    tok = 256 * h + 128 * (k // 3) + start
+    far = [r for r in ranks if r not in ranks_of[k]]
+    near = ranks_of[k]
+    feng = _bits(topo.mask(core, far[0]))
+    for r in far:
+        feng = [e for e in feng if e in _bits(topo.mask(core, r))]
+    neng = [e for e in _bits(topo.mask(core, near[0])) if e not in feng][0:2]
+    rsem = S["arrY%d" % h]
+    trs = []
+    for dst, eng in ((far, feng), (near, neng)):
+        ids = []
+        for r in dst:
+            rid, pid = topo.addr(r, core)
+            ids.append(DstId(rid=rid, pnc=pid))
+        trs.append(RemoteDMATransfer(dst_ids=ids, dma_engine_mask=_mk(eng), remote_sem=rsem, srcs=[T.O[:, lo:BW]],
+                                     dsts=[T.Y[:, tok + lo:tok + BW] for _ in dst], alu_op=0))
+    g.wait_ge(S.s6, 1)
+    g.remote_dma_fused(trs, local_sem=S.lsem)
+    g.wait_ge(S.lsem, sent + len(feng) + len(neng))
+
+
+def rank_program(g, core, T, topo):
+    ranks, chips, ranks_of, agent = _layout(T, topo)
+    for k in range(NCH):
+        if core in ranks_of[k]:
+            _rank(g, core, T, topo, ranks_of, agent, k)
+            return
+        for h in range(2):
+            if agent[k][h] == core:
+                _agent(g, core, T, topo, ranks, ranks_of, agent, k, h)
+                return

@@ -10,22 +10,28 @@ BW = 43
 SW = 44
 HWD = NCH * SW
 STARTS = (0, 43, 85)
+NEAR = 4
 
 F = "float32"
+B = "bfloat16"
 SCRATCH = {
     "xs": ("sbuf", [128, 512], F), "ws": ("sbuf", [128, 128], F), "x2": ("sbuf", [128, 512], F),
     "one3": ("sbuf", [128, 4], F), "stg": ("sbuf", [128, 2 * HWD], F), "Y": ("sbuf", [128, 512], F),
     "L": ("sbuf", [128, 2 * HWD], F), "C": ("sbuf", [128, HWD], F), "R": ("sbuf", [128, HWD], F),
-    "T1": ("sbuf", [128, 3 * SW], F), "T2": ("sbuf", [128, SW], F), "T3": ("sbuf", [128, SW], F),
+    "T3": ("sbuf", [128, SW], F),
     "sst": ("sbuf", [128, 4], F), "sq": ("sbuf", [128, 4], F), "rs": ("sbuf", [128, 4], F),
-    "ones43": ("sbuf", [128, SW], F), "isel": ("sbuf", [128, SW], F), "ones128": ("sbuf", [128, 128], F),
-    "dg": ("sbuf", [128, SW], F), "O": ("sbuf", [128, SW], F),
+    "ones128": ("sbuf", [128, 128], F), "ident": ("sbuf", [128, 128], F),
+    "onesb": ("sbuf", [128, 128], B), "identb": ("sbuf", [128, 128], B), "dgh": ("sbuf", [128, 512], B),
+    "dgl": ("sbuf", [128, 512], B), "rh": ("sbuf", [128, 4], B), "rl": ("sbuf", [128, 4], F),
+    "ssr": ("sbuf", [128, 4], F), "LS": ("sbuf", [128, 8], F), "CS": ("sbuf", [128, 4], F), "RS": ("sbuf", [128, 4 * NCH], F),
     "pc0": ("psum", [128, 512], F), "pc1": ("psum", [128, 512], F), "pc2": ("psum", [128, 512], F),
-    "pc3": ("psum", [128, 512], F), "ps0": ("psum", [128, 512], F), "ps1": ("psum", [128, 512], F),
+    "pc3": ("psum", [128, 512], F), "ps0": ("psum", [128, 512], F),
+    "bc0": ("psum", [128, 512], F), "bc1": ("psum", [128, 512], F),
 }
-SEMAPHORES = ["sw", "sx0", "sx1", "sm", "sq0", "sq1", "pm0", "pm1", "pm2", "pm3", "pss0", "pss1", "cp0", "cp1",
-              "arrL", "arrR", "arrY0", "arrY1", "lsem", "st0", "st1",
-              "si", "cs", "own", "s1", "s2", "s3", "s4", "s5", "s6", "t"]
+SEMAPHORES = ["sw", "sx0", "sx1", "sm", "sq0", "sq1", "pm0", "pm1", "pm2", "pm3", "pss", "cps", "cp0", "cp1",
+              "arrS", "arrRS", "css", "arrL", "arrY0", "arrY1", "lsem", "st0", "st1",
+              "si", "cs", "s1", "s2", "s3", "s4", "s5", "sib", "d0", "d1", "d2", "d3", "b0", "b1", "y0", "y1", "t",
+              "ar0", "ar1", "ar2", "ar3", "ar4", "ar5"]
 
 
 def _bits(m):
@@ -45,15 +51,13 @@ def _layout(T, topo):
             chips.append(key(c))
     dies = sorted(set(topo.die(c) for c in ranks))
     ranks_of = [[c for c in ranks if key(c) == ch] for ch in chips]
-    agent = []
+    agent, courier = [], []
     for ch in chips:
-        row = []
-        for d in dies:
-            cand = [c for c in range(WORLD) if key(c) == ch and topo.die(c) == d and c not in ranks
-                    and all(topo.may_write(c, r) for r in ranks)]
-            row.append(cand[0])
+        cand = [c for c in range(WORLD) if key(c) == ch and c not in ranks and all(topo.may_write(c, r) for r in ranks)]
+        row = [[c for c in cand if topo.die(c) == d][0] for d in dies]
         agent.append(row)
-    return ranks, chips, ranks_of, agent
+        courier.append([c for c in cand if c not in row][0])
+    return ranks, ranks_of, agent, courier
 
 
 def _scatter_plan(k, h, agent, topo):
@@ -68,136 +72,160 @@ def _scatter_plan(k, h, agent, topo):
     return plan
 
 
-def _rank(g, core, T, topo, ranks_of, agent, k):
+def _to_ranks(g, core, T, topo, near, src, dst_ap, sem):
+    far = [r for r in T.cores if r not in near]
+    feng = _bits(topo.mask(core, far[0]))
+    for r in far:
+        feng = [e for e in feng if e in _bits(topo.mask(core, r))]
+    neng = [e for e in _bits(topo.mask(core, near[0])) if e not in feng][0:NEAR]
+    trs = []
+    for grp, eng in ((far, feng), (near, neng)):
+        ids = []
+        for r in grp:
+            rid, pid = topo.addr(r, core)
+            ids.append(DstId(rid=rid, pnc=pid))
+        trs.append(RemoteDMATransfer(dst_ids=ids, dma_engine_mask=_mk(eng), remote_sem=sem, srcs=[src],
+                                     dsts=[dst_ap for _ in grp], alu_op=0))
+    g.remote_dma_fused(trs, local_sem=T.sem.lsem)
+    return len(feng) + len(neng)
+
+
+def _rank(g, core, T, topo, ranks_of, agent, courier, k):
     S = T.sem
+    A = AluOpType
     i = ranks_of[k].index(core)
     Act = ActivationFunctionType
     g.sync.dma_start(T.ws[:], T.w[:]).then_inc(S.sw, 16)
     g.scalar.dma_start(T.xs[:, 0:256], T.x[:, 0:256]).then_inc(S.sx0, 16)
     g.sync.dma_start(T.xs[:, 256:512], T.x[:, 256:512]).then_inc(S.sx1, 16)
     g.vector.memset(T.one3[:], 1.0).then_inc(S.sm, 1)
+    g.vector.memset(T.stg[:, BW:2 * HWD:SW], 0.0).then_inc(S.sm, 1)
+    g.vector.memset(T.ones128[:], 1.0).then_inc(S.sm, 1)
+    g.vector.memset(T.onesb[:], 1.0).then_inc(S.sm, 1)
+    g.wait_ge(S.sm, 4)
+    g.affine_select(T.ident[:], T.ones128[:], [[-1, 128]], A.is_equal, 0.0, 0, 1).then_inc(S.si, 1)
+    g.vector.wait_ge(S.si, 1)
+    g.vector.tensor_copy(T.identb[:], T.ident[:]).then_inc(S.sib, 1)
     for h in range(2):
         g.scalar.wait_ge(S["sx%d" % h], 16)
         g.scalar.activation(T.x2[:, 256 * h:256 * h + 256], T.xs[:, 256 * h:256 * h + 256], Act.Square).then_inc(S["sq%d" % h], 1)
     g.tensor.wait_ge(S.sw, 16)
-    for h in range(2):
-        g.tensor.wait_ge(S["sx%d" % h], 16)
-        for c in (2 * h, 2 * h + 1):
-            g.tensor.matmul(T["pc%d" % c][:, 0:128], T.ws[:], T.xs[:, 128 * c:128 * c + 128], True, True).then_inc(S["pm%d" % c], 1)
-        if h == 0:
-            g.tensor.wait_ge(S.sm, 1)
-        g.tensor.wait_ge(S["sq%d" % h], 1)
-        for cc in range(2):
-            c = 2 * h + cc
-            g.tensor.matmul(T["ps%d" % h][:, 3 * cc:3 * cc + 3], T.x2[:, 128 * c:128 * c + 128], T.one3[:, 0:3], True, True).then_inc(S["pss%d" % h], 1)
-    for h in range(2):
-        cp = S["cp%d" % h]
-        c = 2 * h
-        g.vector.wait_ge(S["pm%d" % c], 1)
+    for c in range(4):
+        g.tensor.wait_ge(S["sx%d" % (c // 2)], 16)
+        g.tensor.matmul(T["pc%d" % c][:, 0:128], T.ws[:], T.xs[:, 128 * c:128 * c + 128], True, True).then_inc(S["pm%d" % c], 1)
+    g.tensor.wait_ge(S.sm, 4)
+    for c in range(4):
+        g.tensor.wait_ge(S["sq%d" % (c // 2)], 1)
+        g.tensor.matmul(T.ps0[:, c:c + 1], T.x2[:, 128 * c:128 * c + 128], T.one3[:, 0:1], True, True).then_inc(S.pss, 1)
+    for c in range(4):
+        q = g.vector if c % 2 == 0 else g.scalar
+        q.wait_ge(S["pm%d" % c], 1)
         for j in range(3):
             s = SW * (3 * c + j)
-            g.vector.tensor_copy(T.stg[:, s:s + BW], T["pc%d" % c][:, STARTS[j]:STARTS[j] + BW]).then_inc(cp, 1)
-        c = 2 * h + 1
-        g.scalar.wait_ge(S["pm%d" % c], 1)
-        for j in range(3):
-            s = SW * (3 * c + j)
-            g.scalar.activation(T.stg[:, s:s + BW], T["pc%d" % c][:, STARTS[j]:STARTS[j] + BW], Act.Copy).then_inc(cp, 1)
-        g.vector.wait_ge(S["pss%d" % h], 2)
-        g.vector.tensor_copy(T.stg[:, HWD * h + BW:HWD * h + HWD:SW], T["ps%d" % h][:, 0:6]).then_inc(cp, 1)
+            src = T["pc%d" % c][:, STARTS[j]:STARTS[j] + BW]
+            if c % 2 == 0:
+                q.tensor_copy(T.stg[:, s:s + BW], src).then_inc(S["cp%d" % (c // 2)], 1)
+            else:
+                q.activation(T.stg[:, s:s + BW], src, Act.Copy).then_inc(S["cp%d" % (c // 2)], 1)
+    g.vector.wait_ge(S.pss, 4)
+    g.vector.tensor_copy(T.ssr[:], T.ps0[:, 0:4]).then_inc(S.cps, 1)
+    mall = topo.mask(core, agent[k][0]) & topo.mask(core, agent[k][1]) & topo.mask(core, courier[k])
+    m = _mk(_bits(mall)[0:8])
     for h in range(2):
-        a = agent[k][h]
-        rid, pid = topo.addr(a, core)
-        m = _mk(_bits(topo.mask(core, a))[0:8])
-        g.wait_ge(S["cp%d" % h], 7)
+        rid, pid = topo.addr(agent[k][h], core)
+        g.wait_ge(S["cp%d" % h], 6)
         g.remote_dma(T.L[:, HWD * i:HWD * i + HWD], T.stg[:, HWD * h:HWD * h + HWD], S.arrL, S.lsem, pid, rid, m)
-    need = 8 * (NCH - 1) + 2
-    g.sync.wait_ge(S.arrY0, need)
-    g.sync.dma_start(T.y[:, 0:256], T.Y[:, 0:256]).then_inc(S.st0, 16)
-    g.scalar.wait_ge(S.arrY1, need)
-    g.scalar.dma_start(T.y[:, 256:512], T.Y[:, 256:512]).then_inc(S.st1, 16)
-    g.wait_ge(S.lsem, 16)
+    rid, pid = topo.addr(courier[k], core)
+    g.wait_ge(S.cps, 1)
+    g.remote_dma(T.LS[:, 4 * i:4 * i + 4], T.ssr[:], S.arrS, S.lsem, pid, rid, m)
+    g.vector.wait_ge(S.arrRS, 8 * (NCH - 1) + NEAR)
+    for c in range(4):
+        g.vector.tensor_reduce(T.sst[:, c:c + 1], T.RS[:, c:4 * NCH:4], AxisListType.X, A.add).then_inc(S.s1, 1)
+    g.scalar.wait_ge(S.s1, 4)
+    g.scalar.activation(T.sq[:], T.sst[:], Act.Sqrt, bias=EPS, scale=1.0 / D).then_inc(S.s2, 1)
+    g.vector.wait_ge(S.s2, 1)
+    g.vector.reciprocal(T.rs[:], T.sq[:]).then_inc(S.s3, 1)
+    g.vector.wait_ge(S.s3, 1)
+    g.vector.tensor_copy(T.rh[:], T.rs[:]).then_inc(S.s4, 1)
+    g.vector.wait_ge(S.s4, 1)
+    g.vector.tensor_tensor(T.rl[:], T.rs[:], T.rh[:], A.subtract).then_inc(S.s5, 1)
+    g.vector.wait_ge(S.sib, 1)
+    g.scalar.wait_ge(S.s5, 1)
+    g.scalar.wait_ge(S.sib, 1)
+    for c in range(4):
+        cs = slice(128 * c, 128 * c + 128)
+        out = T["bc%d" % (c // 2)][:, 128 * (c % 2):128 * (c % 2) + 128]
+        g.vector.tensor_scalar(T.dgh[:, cs], T.identb[:], T.rh[:, c:c + 1], None, A.mult).then_inc(S["d%d" % c], 1)
+        g.scalar.activation(T.dgl[:, cs], T.identb[:], Act.Copy, scale=T.rl[:, c:c + 1]).then_inc(S["d%d" % c], 1)
+        g.tensor.wait_ge(S["d%d" % c], 2)
+        g.tensor.matmul(out, T.onesb[:], T.dgh[:, cs], True, False)
+        g.tensor.matmul(out, T.onesb[:], T.dgl[:, cs], False, True).then_inc(S["b%d" % (c // 2)], 1)
+    need = 8 * (NCH - 1) + NEAR
+    for h, q in ((0, g.sync), (1, g.scalar)):
+        hs = slice(256 * h, 256 * h + 256)
+        g.vector.wait_ge(S["b%d" % h], 2)
+        g.vector.wait_ge(S["arrY%d" % h], need)
+        g.vector.tensor_tensor(T.Y[:, hs], T.Y[:, hs], T["bc%d" % h][:, 0:256], A.mult).then_inc(S["y%d" % h], 1)
+        q.wait_ge(S["y%d" % h], 1)
+        q.dma_start(T.y[:, hs], T.Y[:, hs]).then_inc(S["st%d" % h], 16)
+    g.wait_ge(S.lsem, 24)
     g.wait_ge(S.st0, 16)
     g.wait_ge(S.st1, 16)
 
 
-def _agent(g, core, T, topo, ranks, ranks_of, agent, k, h):
+def _courier(g, core, T, topo, ranks_of, k):
+    S = T.sem
+    g.vector.wait_ge(S.arrS, 16)
+    g.vector.tensor_tensor(T.CS[:], T.LS[:, 0:4], T.LS[:, 4:8], AluOpType.add).then_inc(S.css, 1)
+    g.wait_ge(S.css, 1)
+    g.wait_ge(S.lsem, _to_ranks(g, core, T, topo, ranks_of[k], T.CS[:], T.RS[:, 4 * k:4 * k + 4], S.arrRS))
+
+
+def _agent(g, core, T, topo, ranks_of, agent, k, h):
     S = T.sem
     A = AluOpType
-    start = STARTS[k % 3]
     own = slice(SW * k, SW * k + SW)
-    g.vector.memset(T.ones43[:, 0:BW], 1.0).then_inc(S.sm, 1)
-    g.vector.memset(T.ones128[:], 1.0).then_inc(S.sm, 1)
-    g.wait_ge(S.sm, 2)
-    g.affine_select(T.isel[:, 0:BW], T.ones43[:, 0:BW], [[-1, BW]], A.is_equal, 0.0, -start, 1).then_inc(S.si, 1)
+    plan = _scatter_plan(k, h, agent, topo)
+    acc = T.pc0[:, 0:SW]
     g.vector.wait_ge(S.arrL, 16)
     g.vector.tensor_tensor(T.C[:], T.L[:, 0:HWD], T.L[:, HWD:2 * HWD], A.add).then_inc(S.cs, 1)
-    g.vector.tensor_tensor(T.R[:, own], T.L[:, own], T.L[:, HWD + SW * k:HWD + SW * k + SW], A.add).then_inc(S.own, 1)
-    plan = _scatter_plan(k, h, agent, topo)
+    g.vector.tensor_tensor(acc, T.L[:, own], T.L[:, HWD + SW * k:HWD + SW * k + SW], A.add).then_inc(S.t, 1)
     g.wait_ge(S.cs, 1)
     trs = []
     for b, eng in plan[:4]:
         rid, pid = topo.addr(agent[b][h], core)
-        trs.append(RemoteDMATransfer(dst_ids=[DstId(rid=rid, pnc=pid)], dma_engine_mask=_mk(eng), remote_sem=S.arrR,
+        trs.append(RemoteDMATransfer(dst_ids=[DstId(rid=rid, pnc=pid)], dma_engine_mask=_mk(eng), remote_sem=S["ar%d" % k],
                                      srcs=[T.C[:, SW * b:SW * b + SW]], dsts=[T.R[:, own]], alu_op=0))
     g.remote_dma_fused(trs, local_sem=S.lsem)
     b, eng = plan[4]
     rid, pid = topo.addr(agent[b][h], core)
-    g.remote_dma(T.R[:, own], T.C[:, SW * b:SW * b + SW], S.arrR, S.lsem, pid, rid, _mk(eng))
+    g.remote_dma(T.R[:, own], T.C[:, SW * b:SW * b + SW], S["ar%d" % k], S.lsem, pid, rid, _mk(eng))
     sent = sum(len(e) for _, e in plan)
-    need = 0
+    src = []
     for kk in range(NCH):
         if kk != k:
-            need += sum(len(e) for b2, e in _scatter_plan(kk, h, agent, topo) if b2 == k)
-    g.vector.wait_ge(S.arrR, need)
-    g.vector.wait_ge(S.own, 1)
-    g.vector.tensor_reduce(T.sst[:, 0:1], T.R[:, BW:HWD:SW], AxisListType.X, A.add).then_inc(S.s1, 1)
-    g.scalar.wait_ge(S.s1, 1)
-    g.scalar.activation(T.sq[:, 0:1], T.sst[:, 0:1], ActivationFunctionType.Sqrt, bias=EPS, scale=1.0 / D).then_inc(S.s2, 1)
-    g.vector.tensor_tensor(T.T1[:], T.R[:, 0:3 * SW], T.R[:, 3 * SW:6 * SW], A.add).then_inc(S.t, 1)
-    g.vector.wait_ge(S.t, 1)
-    g.vector.tensor_tensor(T.T2[:], T.T1[:, 0:SW], T.T1[:, SW:2 * SW], A.add).then_inc(S.t, 1)
-    g.vector.wait_ge(S.t, 2)
-    g.vector.tensor_tensor(T.T3[:], T.T2[:], T.T1[:, 2 * SW:3 * SW], A.add).then_inc(S.t, 1)
-    g.vector.wait_ge(S.s2, 1)
-    g.vector.reciprocal(T.rs[:, 0:1], T.sq[:, 0:1]).then_inc(S.s3, 1)
-    g.vector.wait_ge(S.s3, 1)
-    g.vector.wait_ge(S.si, 1)
-    g.vector.tensor_scalar(T.dg[:, 0:BW], T.isel[:, 0:BW], T.rs[:, 0:1], None, A.mult).then_inc(S.s4, 1)
-    g.tensor.wait_ge(S.sm, 2)
-    g.tensor.wait_ge(S.s4, 1)
-    g.tensor.matmul(T.pc0[:, 0:BW], T.ones128[:], T.dg[:, 0:BW], True, True).then_inc(S.s5, 1)
-    g.vector.wait_ge(S.s5, 1)
-    g.vector.wait_ge(S.t, 3)
-    g.vector.tensor_tensor(T.O[:, 0:BW], T.T3[:, 0:BW], T.pc0[:, 0:BW], A.mult).then_inc(S.s6, 1)
+            pl = _scatter_plan(kk, h, agent, topo)
+            pos = [j for j, (b2, e) in enumerate(pl) if b2 == k][0]
+            src.append((1 if pos == 4 else 0, 0 if topo.same_plane(core, agent[kk][h]) else 1, kk, len(pl[pos][1])))
+    src.sort()
+    for n, (_, _, kk, cnt) in enumerate(src):
+        g.vector.wait_ge(S["ar%d" % kk], cnt)
+        g.vector.wait_ge(S.t, n + 1)
+        out = T.T3[:] if n == len(src) - 1 else acc
+        g.vector.tensor_tensor(out, acc, T.R[:, SW * kk:SW * kk + SW], A.add).then_inc(S.t, 1)
     lo = 1 if k % 3 == 2 else 0
-    tok = 256 * h + 128 * (k // 3) + start
-    far = [r for r in ranks if r not in ranks_of[k]]
-    near = ranks_of[k]
-    feng = _bits(topo.mask(core, far[0]))
-    for r in far:
-        feng = [e for e in feng if e in _bits(topo.mask(core, r))]
-    neng = [e for e in _bits(topo.mask(core, near[0])) if e not in feng][0:2]
-    rsem = S["arrY%d" % h]
-    trs = []
-    for dst, eng in ((far, feng), (near, neng)):
-        ids = []
-        for r in dst:
-            rid, pid = topo.addr(r, core)
-            ids.append(DstId(rid=rid, pnc=pid))
-        trs.append(RemoteDMATransfer(dst_ids=ids, dma_engine_mask=_mk(eng), remote_sem=rsem, srcs=[T.O[:, lo:BW]],
-                                     dsts=[T.Y[:, tok + lo:tok + BW] for _ in dst], alu_op=0))
-    g.wait_ge(S.s6, 1)
-    g.remote_dma_fused(trs, local_sem=S.lsem)
-    g.wait_ge(S.lsem, sent + len(feng) + len(neng))
+    tok = 256 * h + 128 * (k // 3) + STARTS[k % 3]
+    g.wait_ge(S.t, len(src) + 1)
+    sent += _to_ranks(g, core, T, topo, ranks_of[k], T.T3[:, lo:BW], T.Y[:, tok + lo:tok + BW], S["arrY%d" % h])
+    g.wait_ge(S.lsem, sent)
 
 
 def rank_program(g, core, T, topo):
-    ranks, chips, ranks_of, agent = _layout(T, topo)
+    ranks, ranks_of, agent, courier = _layout(T, topo)
     for k in range(NCH):
         if core in ranks_of[k]:
-            _rank(g, core, T, topo, ranks_of, agent, k)
-            return
-        for h in range(2):
-            if agent[k][h] == core:
-                _agent(g, core, T, topo, ranks, ranks_of, agent, k, h)
-                return
+            _rank(g, core, T, topo, ranks_of, agent, courier, k)
+        elif core == courier[k]:
+            _courier(g, core, T, topo, ranks_of, k)
+        elif core in agent[k]:
+            _agent(g, core, T, topo, ranks_of, agent, k, agent[k].index(core))

@@ -8,6 +8,7 @@ EPS = 0.01
 NCH = 6
 BW = 43
 SW = 44
+QW = 3 * SW
 HWD = NCH * SW
 STARTS = (0, 43, 85)
 NEAR = 4
@@ -17,6 +18,7 @@ B = "bfloat16"
 SCRATCH = {
     "xs": ("sbuf", [128, 512], F), "ws": ("sbuf", [128, 128], F), "x2": ("sbuf", [128, 512], F),
     "one3": ("sbuf", [128, 4], F), "stg": ("sbuf", [128, 2 * HWD], F), "Y": ("sbuf", [128, 512], F),
+    "Yo": ("sbuf", [128, 512], F),
     "L": ("sbuf", [128, 2 * HWD], F), "C": ("sbuf", [128, HWD], F), "R": ("sbuf", [128, HWD], F),
     "T3": ("sbuf", [128, SW], F),
     "sst": ("sbuf", [128, 4], F), "sq": ("sbuf", [128, 4], F), "rs": ("sbuf", [128, 4], F),
@@ -28,10 +30,10 @@ SCRATCH = {
     "pc3": ("psum", [128, 512], F), "ps0": ("psum", [128, 512], F),
     "bc0": ("psum", [128, 512], F), "bc1": ("psum", [128, 512], F),
 }
-SEMAPHORES = ["sw", "sx0", "sx1", "sm", "sq0", "sq1", "pm0", "pm1", "pm2", "pm3", "pss", "cps", "cp0", "cp1",
-              "arrS", "arrRS", "css", "arrL", "arrY0", "arrY1", "lsem", "st0", "st1",
-              "si", "cs", "s1", "s2", "s3", "s4", "s5", "sib", "d0", "d1", "d2", "d3", "b0", "b1", "y0", "y1", "t",
-              "ar0", "ar1", "ar2", "ar3", "ar4", "ar5"]
+SEMAPHORES = ["sw", "sx0", "sx1", "sm", "sq0", "sq1", "pm0", "pm1", "pm2", "pm3", "pss", "cps", "cp0", "cp1", "cp2", "cp3",
+              "arrS", "arrRS", "css", "aL0", "aL1", "aY0", "aY1", "aX0", "aX1", "lsem", "st0", "st1", "st2", "st3",
+              "si", "cs0", "cs1", "s1", "s2", "s3", "s4", "s5", "sib", "d0", "d1", "d2", "d3", "b0", "b1",
+              "y0", "y1", "y2", "y3", "t", "ar0", "ar1", "ar2", "ar3", "ar4", "ar5"]
 
 
 def _bits(m):
@@ -51,46 +53,69 @@ def _layout(T, topo):
             chips.append(key(c))
     dies = sorted(set(topo.die(c) for c in ranks))
     ranks_of = [[c for c in ranks if key(c) == ch] for ch in chips]
-    agent, courier = [], []
-    for ch in chips:
-        cand = [c for c in range(WORLD) if key(c) == ch and c not in ranks and all(topo.may_write(c, r) for r in ranks)]
+    seen, targets = [], []
+    for a in range(NCH):
+        if a not in seen:
+            b = [b for b in range(a + 1, NCH) if b not in seen and topo.same_plane(ranks_of[a][0], ranks_of[b][0])][0]
+            seen += [a, b]
+            targets.append(ranks_of[a] + ranks_of[b])
+    agent, courier, recv = [], [], []
+    for k, ch in enumerate(chips):
+        helpers = [c for c in range(WORLD) if key(c) == ch and c not in ranks]
+        cand = [c for c in helpers if all(topo.may_write(c, r) for r in ranks)]
         row = [[c for c in cand if topo.die(c) == d][0] for d in dies]
         agent.append(row)
-        courier.append([c for c in cand if c not in row][0])
-    return ranks, ranks_of, agent, courier
+        recv.append([[r for r in ranks_of[k] if topo.die(r) == d][0] for d in dies])
+        spare = [c for c in helpers if c not in row]
+        spare.sort(key=lambda c: sum(1 for r in ranks if topo.may_write(c, r)))
+        able = lambda pool, q, used: [c for c in pool if c not in used and c not in targets[q]
+                                      and all(topo.may_write(c, r) for r in targets[q])]
+        used, cr = [], {}
+        for q in sorted(range(len(targets)), key=lambda q: len(able(spare, q, []))):
+            a = able(spare, q, used) or able(ranks_of[k], q, used)
+            cr[q] = a[0]
+            used.append(a[0])
+        courier.append(cr)
+    return ranks, ranks_of, agent, courier, recv, targets
 
 
-def _scatter_plan(k, h, agent, topo):
+def _common(core, dests, topo):
+    eng = _bits(topo.mask(core, dests[0]))
+    for d in dests:
+        eng = [e for e in eng if e in _bits(topo.mask(core, d))]
+    return eng
+
+
+def _send(g, core, T, topo, dests, src, dst_ap, sem, eng):
+    ids = []
+    for r in dests:
+        rid, pid = topo.addr(r, core)
+        ids.append(DstId(rid=rid, pnc=pid))
+    g.remote_dma_fused([RemoteDMATransfer(dst_ids=ids, dma_engine_mask=_mk(eng), remote_sem=sem, srcs=[src],
+                                          dsts=[dst_ap for _ in dests], alu_op=0)], local_sem=T.sem.lsem)
+    return len(eng)
+
+
+def _scatter_plan(k, h, e, agent, topo):
     me = agent[k][h]
-    others = [(k + j) % NCH for j in range(1, NCH)]
+    others = [b for b in range(3 * e, 3 * e + 3) if b != k]
     others.sort(key=lambda b: 1 if topo.same_plane(me, agent[b][h]) else 0)
-    eng = _bits(topo.mask(me, agent[others[0]][h]))
-    for b in others:
-        eng = [e for e in eng if e in _bits(topo.mask(me, agent[b][h]))]
-    plan = [(b, eng[2 * j:2 * j + 2]) for j, b in enumerate(others[:4])]
-    plan.append((others[4], eng))
-    return plan
+    eng = _common(me, [agent[b][h] for b in range(NCH) if b != k], topo)
+    n = len(eng)
+    if len(others) == 2:
+        cut = [eng[0:n // 2], eng[n // 2:n]]
+    else:
+        cut = [eng[0:n // 2], eng[n // 2:3 * n // 4], eng[3 * n // 4:n]]
+    return [(b, cut[j]) for j, b in enumerate(others)]
 
 
-def _to_ranks(g, core, T, topo, near, src, dst_ap, sem):
-    far = [r for r in T.cores if r not in near]
-    feng = _bits(topo.mask(core, far[0]))
-    for r in far:
-        feng = [e for e in feng if e in _bits(topo.mask(core, r))]
-    neng = [e for e in _bits(topo.mask(core, near[0])) if e not in feng][0:NEAR]
-    trs = []
-    for grp, eng in ((far, feng), (near, neng)):
-        ids = []
-        for r in grp:
-            rid, pid = topo.addr(r, core)
-            ids.append(DstId(rid=rid, pnc=pid))
-        trs.append(RemoteDMATransfer(dst_ids=ids, dma_engine_mask=_mk(eng), remote_sem=sem, srcs=[src],
-                                     dsts=[dst_ap for _ in grp], alu_op=0))
-    g.remote_dma_fused(trs, local_sem=T.sem.lsem)
-    return len(feng) + len(neng)
+def _last_engines(k, h, agent, recv, topo):
+    far = _common(agent[k][h], [recv[kk][h] for kk in range(NCH) if kk != k], topo)
+    near = [e for e in _common(agent[k][h], [recv[k][h]], topo) if e not in far][0:NEAR]
+    return far, near
 
 
-def _rank(g, core, T, topo, ranks_of, agent, courier, k):
+def _rank(g, core, T, topo, ranks_of, agent, courier, recv, targets, k):
     S = T.sem
     A = AluOpType
     i = ranks_of[k].index(core)
@@ -121,24 +146,53 @@ def _rank(g, core, T, topo, ranks_of, agent, courier, k):
         q = g.vector if c % 2 == 0 else g.scalar
         q.wait_ge(S["pm%d" % c], 1)
         for j in range(3):
-            s = SW * (3 * c + j)
+            s = HWD * (c % 2) + QW * (c // 2) + SW * j
             src = T["pc%d" % c][:, STARTS[j]:STARTS[j] + BW]
             if c % 2 == 0:
-                q.tensor_copy(T.stg[:, s:s + BW], src).then_inc(S["cp%d" % (c // 2)], 1)
+                q.tensor_copy(T.stg[:, s:s + BW], src).then_inc(S["cp%d" % c], 1)
             else:
-                q.activation(T.stg[:, s:s + BW], src, Act.Copy).then_inc(S["cp%d" % (c // 2)], 1)
+                q.activation(T.stg[:, s:s + BW], src, Act.Copy).then_inc(S["cp%d" % c], 1)
     g.vector.wait_ge(S.pss, 4)
     g.vector.tensor_copy(T.ssr[:], T.ps0[:, 0:4]).then_inc(S.cps, 1)
-    mall = topo.mask(core, agent[k][0]) & topo.mask(core, agent[k][1]) & topo.mask(core, courier[k])
-    m = _mk(_bits(mall)[0:8])
-    for h in range(2):
+    partner = ranks_of[k][1 - i]
+    crs = [courier[k][q] for q in sorted(courier[k]) if courier[k][q] != core]
+    em = _common(core, agent[k] + crs + [partner], topo)[0:8]
+    m = _mk(em)
+    sent = 0
+    for c in range(4):
+        h, e = c % 2, c // 2
         rid, pid = topo.addr(agent[k][h], core)
-        g.wait_ge(S["cp%d" % h], 6)
-        g.remote_dma(T.L[:, HWD * i:HWD * i + HWD], T.stg[:, HWD * h:HWD * h + HWD], S.arrL, S.lsem, pid, rid, m)
-    rid, pid = topo.addr(courier[k], core)
+        g.wait_ge(S["cp%d" % c], 3)
+        g.remote_dma(T.L[:, HWD * i + QW * e:HWD * i + QW * e + QW], T.stg[:, HWD * h + QW * e:HWD * h + QW * e + QW],
+                     S["aL%d" % e], S.lsem, pid, rid, m)
+        sent += len(em)
     g.wait_ge(S.cps, 1)
-    g.remote_dma(T.LS[:, 4 * i:4 * i + 4], T.ssr[:], S.arrS, S.lsem, pid, rid, m)
-    g.vector.wait_ge(S.arrRS, 8 * (NCH - 1) + NEAR)
+    sent += _send(g, core, T, topo, crs, T.ssr[:], T.LS[:, 4 * i:4 * i + 4], S.arrS, em)
+    for q in sorted(courier[k]):
+        if courier[k][q] == core:
+            o = 1 - i
+            g.vector.wait_ge(S.arrS, len(em))
+            g.vector.wait_ge(S.cps, 1)
+            g.vector.tensor_tensor(T.CS[:], T.ssr[:], T.LS[:, 4 * o:4 * o + 4], A.add).then_inc(S.css, 1)
+            g.wait_ge(S.css, 1)
+            sent += _send(g, core, T, topo, targets[q], T.CS[:], T.RS[:, 4 * k:4 * k + 4], S.arrRS,
+                          _common(core, targets[q], topo))
+    hown = recv[k].index(core)
+    need = []
+    for e in range(2):
+        n = 0
+        for b in range(3 * e, 3 * e + 3):
+            far, near = _last_engines(b, hown, agent, recv, topo)
+            n += len(near) if b == k else len(far)
+        need.append(n)
+    rid, pid = topo.addr(partner, core)
+    for e in range(2):
+        cs = slice(128 * (hown + 2 * e), 128 * (hown + 2 * e) + 128)
+        g.wait_ge(S["aY%d" % e], need[e])
+        g.remote_dma(T.Y[:, cs], T.Y[:, cs], S["aX%d" % e], S.lsem, pid, rid, m)
+        sent += len(em)
+    myq = [q for q in range(len(targets)) if core in targets[q]][0]
+    g.vector.wait_ge(S.arrRS, sum(len(_common(courier[kk][myq], targets[myq], topo)) for kk in range(NCH)))
     for c in range(4):
         g.vector.tensor_reduce(T.sst[:, c:c + 1], T.RS[:, c:4 * NCH:4], AxisListType.X, A.add).then_inc(S.s1, 1)
     g.scalar.wait_ge(S.s1, 4)
@@ -160,53 +214,59 @@ def _rank(g, core, T, topo, ranks_of, agent, courier, k):
         g.tensor.wait_ge(S["d%d" % c], 2)
         g.tensor.matmul(out, T.onesb[:], T.dgh[:, cs], True, False)
         g.tensor.matmul(out, T.onesb[:], T.dgl[:, cs], False, True).then_inc(S["b%d" % (c // 2)], 1)
-    need = 8 * (NCH - 1) + NEAR
-    for h, q in ((0, g.sync), (1, g.scalar)):
-        hs = slice(256 * h, 256 * h + 256)
-        g.vector.wait_ge(S["b%d" % h], 2)
-        g.vector.wait_ge(S["arrY%d" % h], need)
-        g.vector.tensor_tensor(T.Y[:, hs], T.Y[:, hs], T["bc%d" % h][:, 0:256], A.mult).then_inc(S["y%d" % h], 1)
-        q.wait_ge(S["y%d" % h], 1)
-        q.dma_start(T.y[:, hs], T.Y[:, hs]).then_inc(S["st%d" % h], 16)
-    g.wait_ge(S.lsem, 24)
-    g.wait_ge(S.st0, 16)
-    g.wait_ge(S.st1, 16)
+    for e in range(2):
+        for h, q in ((hown, g.sync), (1 - hown, g.scalar)):
+            c = h + 2 * e
+            cs = slice(128 * c, 128 * c + 128)
+            g.vector.wait_ge(S["b%d" % (c // 2)], 2)
+            if h == hown:
+                g.vector.wait_ge(S["aY%d" % e], need[e])
+            else:
+                g.vector.wait_ge(S["aX%d" % e], len(em))
+            g.vector.tensor_tensor(T.Yo[:, cs], T.Y[:, cs], T["bc%d" % (c // 2)][:, 128 * (c % 2):128 * (c % 2) + 128],
+                                   A.mult).then_inc(S["y%d" % c], 1)
+            q.wait_ge(S["y%d" % c], 1)
+            q.dma_start(T.y[:, cs], T.Yo[:, cs]).then_inc(S["st%d" % c], 16)
+    g.wait_ge(S.lsem, sent)
+    for c in range(4):
+        g.wait_ge(S["st%d" % c], 16)
 
 
-def _courier(g, core, T, topo, ranks_of, k):
+def _courier(g, core, T, topo, tg, k):
     S = T.sem
     g.vector.wait_ge(S.arrS, 16)
     g.vector.tensor_tensor(T.CS[:], T.LS[:, 0:4], T.LS[:, 4:8], AluOpType.add).then_inc(S.css, 1)
     g.wait_ge(S.css, 1)
-    g.wait_ge(S.lsem, _to_ranks(g, core, T, topo, ranks_of[k], T.CS[:], T.RS[:, 4 * k:4 * k + 4], S.arrRS))
+    g.wait_ge(S.lsem, _send(g, core, T, topo, tg, T.CS[:], T.RS[:, 4 * k:4 * k + 4], S.arrRS, _common(core, tg, topo)))
 
 
-def _agent(g, core, T, topo, ranks_of, agent, k, h):
+def _agent(g, core, T, topo, ranks_of, agent, recv, k, h):
     S = T.sem
     A = AluOpType
     own = slice(SW * k, SW * k + SW)
-    plan = _scatter_plan(k, h, agent, topo)
+    eo = k // 3
     acc = T.pc0[:, 0:SW]
-    g.vector.wait_ge(S.arrL, 16)
-    g.vector.tensor_tensor(T.C[:], T.L[:, 0:HWD], T.L[:, HWD:2 * HWD], A.add).then_inc(S.cs, 1)
-    g.vector.tensor_tensor(acc, T.L[:, own], T.L[:, HWD + SW * k:HWD + SW * k + SW], A.add).then_inc(S.t, 1)
-    g.wait_ge(S.cs, 1)
-    trs = []
-    for b, eng in plan[:4]:
-        rid, pid = topo.addr(agent[b][h], core)
-        trs.append(RemoteDMATransfer(dst_ids=[DstId(rid=rid, pnc=pid)], dma_engine_mask=_mk(eng), remote_sem=S["ar%d" % k],
-                                     srcs=[T.C[:, SW * b:SW * b + SW]], dsts=[T.R[:, own]], alu_op=0))
-    g.remote_dma_fused(trs, local_sem=S.lsem)
-    b, eng = plan[4]
-    rid, pid = topo.addr(agent[b][h], core)
-    g.remote_dma(T.R[:, own], T.C[:, SW * b:SW * b + SW], S["ar%d" % k], S.lsem, pid, rid, _mk(eng))
-    sent = sum(len(e) for _, e in plan)
+    sent = 0
+    for e in range(2):
+        g.vector.wait_ge(S["aL%d" % e], 16)
+        g.vector.tensor_tensor(T.C[:, QW * e:QW * e + QW], T.L[:, QW * e:QW * e + QW],
+                               T.L[:, HWD + QW * e:HWD + QW * e + QW], A.add).then_inc(S["cs%d" % e], 1)
+        if e == eo:
+            g.vector.tensor_tensor(acc, T.L[:, own], T.L[:, HWD + SW * k:HWD + SW * k + SW], A.add).then_inc(S.t, 1)
+        g.wait_ge(S["cs%d" % e], 1)
+        trs = []
+        for b, eng in _scatter_plan(k, h, e, agent, topo):
+            rid, pid = topo.addr(agent[b][h], core)
+            trs.append(RemoteDMATransfer(dst_ids=[DstId(rid=rid, pnc=pid)], dma_engine_mask=_mk(eng),
+                                         remote_sem=S["ar%d" % k], srcs=[T.C[:, SW * b:SW * b + SW]], dsts=[T.R[:, own]],
+                                         alu_op=0))
+            sent += len(eng)
+        g.remote_dma_fused(trs, local_sem=S.lsem)
     src = []
     for kk in range(NCH):
         if kk != k:
-            pl = _scatter_plan(kk, h, agent, topo)
-            pos = [j for j, (b2, e) in enumerate(pl) if b2 == k][0]
-            src.append((1 if pos == 4 else 0, 0 if topo.same_plane(core, agent[kk][h]) else 1, kk, len(pl[pos][1])))
+            cnt = [len(eng) for b, eng in _scatter_plan(kk, h, eo, agent, topo) if b == k][0]
+            src.append((-cnt, 0 if topo.same_plane(core, agent[kk][h]) else 1, kk, cnt))
     src.sort()
     for n, (_, _, kk, cnt) in enumerate(src):
         g.vector.wait_ge(S["ar%d" % kk], cnt)
@@ -214,18 +274,23 @@ def _agent(g, core, T, topo, ranks_of, agent, k, h):
         out = T.T3[:] if n == len(src) - 1 else acc
         g.vector.tensor_tensor(out, acc, T.R[:, SW * kk:SW * kk + SW], A.add).then_inc(S.t, 1)
     lo = 1 if k % 3 == 2 else 0
-    tok = 256 * h + 128 * (k // 3) + STARTS[k % 3]
+    tok = 128 * (h + 2 * eo) + STARTS[k % 3]
+    far, near = _last_engines(k, h, agent, recv, topo)
     g.wait_ge(S.t, len(src) + 1)
-    sent += _to_ranks(g, core, T, topo, ranks_of[k], T.T3[:, lo:BW], T.Y[:, tok + lo:tok + BW], S["arrY%d" % h])
+    sent += _send(g, core, T, topo, [recv[kk][h] for kk in range(NCH) if kk != k], T.T3[:, lo:BW],
+                  T.Y[:, tok + lo:tok + BW], S["aY%d" % eo], far)
+    sent += _send(g, core, T, topo, [recv[k][h]], T.T3[:, lo:BW], T.Y[:, tok + lo:tok + BW], S["aY%d" % eo], near)
     g.wait_ge(S.lsem, sent)
 
 
 def rank_program(g, core, T, topo):
-    ranks, ranks_of, agent, courier = _layout(T, topo)
+    ranks, ranks_of, agent, courier, recv, targets = _layout(T, topo)
     for k in range(NCH):
         if core in ranks_of[k]:
-            _rank(g, core, T, topo, ranks_of, agent, courier, k)
-        elif core == courier[k]:
-            _courier(g, core, T, topo, ranks_of, k)
+            _rank(g, core, T, topo, ranks_of, agent, courier, recv, targets, k)
         elif core in agent[k]:
-            _agent(g, core, T, topo, ranks_of, agent, k, agent[k].index(core))
+            _agent(g, core, T, topo, ranks_of, agent, recv, k, agent[k].index(core))
+        else:
+            for q in sorted(courier[k]):
+                if courier[k][q] == core:
+                    _courier(g, core, T, topo, targets[q], k)

@@ -8,7 +8,7 @@ EPS = 0.01
 NCH = 6
 BW = 43
 SW = 44
-QW = 3 * SW
+CW = 128
 HWD = NCH * SW
 STARTS = (0, 43, 85)
 NEAR = 4
@@ -17,21 +17,22 @@ F = "float32"
 B = "bfloat16"
 SCRATCH = {
     "xs": ("sbuf", [128, 512], F), "ws": ("sbuf", [128, 128], F), "x2": ("sbuf", [128, 512], F),
-    "one3": ("sbuf", [128, 4], F), "stg": ("sbuf", [128, 2 * HWD], F), "Y": ("sbuf", [128, 512], F),
+    "one3": ("sbuf", [128, 4], F), "stg": ("sbuf", [128, 2 * CW], F), "Y": ("sbuf", [128, 512], F),
     "Yo": ("sbuf", [128, 512], F),
-    "L": ("sbuf", [128, 2 * HWD], F), "C": ("sbuf", [128, HWD], F), "R": ("sbuf", [128, HWD], F),
+    "L": ("sbuf", [128, 2 * CW], F), "C": ("sbuf", [128, 2 * CW], F), "R": ("sbuf", [128, HWD], F),
+    "WA": ("sbuf", [128, 2 * 128], F), "XA": ("sbuf", [128, 2 * CW], F),
     "T3": ("sbuf", [128, SW], F),
     "sst": ("sbuf", [128, 4], F), "sq": ("sbuf", [128, 4], F), "rs": ("sbuf", [128, 4], F),
     "ones128": ("sbuf", [128, 128], F), "ident": ("sbuf", [128, 128], F),
     "onesb": ("sbuf", [128, 128], B), "identb": ("sbuf", [128, 128], B), "dgh": ("sbuf", [128, 512], B),
     "dgl": ("sbuf", [128, 512], B), "rh": ("sbuf", [128, 4], B), "rl": ("sbuf", [128, 4], F),
     "ssr": ("sbuf", [128, 4], F), "LS": ("sbuf", [128, 8], F), "CS": ("sbuf", [128, 4], F), "RS": ("sbuf", [128, 4 * NCH], F),
-    "pc0": ("psum", [128, 512], F), "pc1": ("psum", [128, 512], F), "pc2": ("psum", [128, 512], F),
-    "pc3": ("psum", [128, 512], F), "ps0": ("psum", [128, 512], F),
+    "pc0": ("psum", [128, 512], F), "pc1": ("psum", [128, 512], F), "ps0": ("psum", [128, 512], F),
     "bc0": ("psum", [128, 512], F), "bc1": ("psum", [128, 512], F),
 }
-SEMAPHORES = ["sw", "sx0", "sx1", "sm", "sq0", "sq1", "pm0", "pm1", "pm2", "pm3", "pss", "cps", "cp0", "cp1", "cp2", "cp3",
-              "arrS", "arrRS", "css", "aL0", "aL1", "aY0", "aY1", "aX0", "aX1", "lsem", "st0", "st1", "st2", "st3",
+SEMAPHORES = ["so", "sob", "sw", "sx0", "sx1", "sm", "sq0", "sq1", "pm0", "pm1", "pss", "cps", "cp0", "cp1",
+              "aW", "aR", "pmA",
+              "arrS", "arrRS", "css", "aL0", "aY0", "aY1", "aX0", "aX1", "lsem", "st0", "st1", "st2", "st3",
               "si", "cs0", "cs1", "s1", "s2", "s3", "s4", "s5", "sib", "d0", "d1", "d2", "d3", "b0", "b1",
               "y0", "y1", "y2", "y3", "t", "ar0", "ar1", "ar2", "ar3", "ar4", "ar5"]
 
@@ -86,6 +87,16 @@ def _common(core, dests, topo):
     return eng
 
 
+def _ss_dests(r, k, courier):
+    return [courier[k][q] for q in sorted(courier[k]) if courier[k][q] != r]
+
+
+def _raw_engines(r, k, h, agent, topo):
+    eng = _common(r, agent[k], topo)
+    n = len(eng) // 2
+    return eng[n * h:n * h + n]
+
+
 def _send(g, core, T, topo, dests, src, dst_ap, sem, eng):
     ids = []
     for r in dests:
@@ -96,17 +107,22 @@ def _send(g, core, T, topo, dests, src, dst_ap, sem, eng):
     return len(eng)
 
 
-def _scatter_plan(k, h, e, agent, topo):
-    me = agent[k][h]
-    others = [b for b in range(3 * e, 3 * e + 3) if b != k]
-    others.sort(key=lambda b: 1 if topo.same_plane(me, agent[b][h]) else 0)
-    eng = _common(me, [agent[b][h] for b in range(NCH) if b != k], topo)
-    n = len(eng)
-    if len(others) == 2:
-        cut = [eng[0:n // 2], eng[n // 2:n]]
-    else:
-        cut = [eng[0:n // 2], eng[n // 2:3 * n // 4], eng[3 * n // 4:n]]
-    return [(b, cut[j]) for j, b in enumerate(others)]
+def _scatter_plan(h, e, agent, topo):
+    plan, thirds = {}, {}
+    for k in range(NCH):
+        me = agent[k][h]
+        others = [b for b in range(3 * e, 3 * e + 3) if b != k]
+        eng = _common(me, [agent[b][h] for b in range(NCH) if b != k], topo)
+        n = len(eng)
+        calls = []
+        if len(others) == 3:
+            near = [b for b in others if topo.same_plane(me, agent[b][h])] or others
+            last = min(near, key=lambda b: (thirds.get(b, 0), b))
+            thirds[last] = thirds.get(last, 0) + 1
+            others = [b for b in others if b != last]
+            calls = [[(last, eng)]]
+        plan[k] = [[(others[0], eng[0:n // 2]), (others[1], eng[n // 2:n])]] + calls
+    return plan
 
 
 def _last_engines(k, h, agent, recv, topo):
@@ -121,57 +137,60 @@ def _rank(g, core, T, topo, ranks_of, agent, courier, recv, targets, k):
     i = ranks_of[k].index(core)
     Act = ActivationFunctionType
     g.sync.dma_start(T.ws[:], T.w[:]).then_inc(S.sw, 16)
-    g.scalar.dma_start(T.xs[:, 0:256], T.x[:, 0:256]).then_inc(S.sx0, 16)
-    g.sync.dma_start(T.xs[:, 256:512], T.x[:, 256:512]).then_inc(S.sx1, 16)
+    g.scalar.dma_start(T.xs[:, 256:512], T.x[:, 256:512]).then_inc(S.sx1, 16)
+    g.sync.dma_start(T.xs[:, 0:256], T.x[:, 0:256]).then_inc(S.sx0, 16)
+    g.vector.memset(T.ones128[:], 1.0).then_inc(S.so, 1)
     g.vector.memset(T.one3[:], 1.0).then_inc(S.sm, 1)
-    g.vector.memset(T.stg[:, BW:2 * HWD:SW], 0.0).then_inc(S.sm, 1)
-    g.vector.memset(T.ones128[:], 1.0).then_inc(S.sm, 1)
-    g.vector.memset(T.onesb[:], 1.0).then_inc(S.sm, 1)
-    g.wait_ge(S.sm, 4)
+    g.wait_ge(S.so, 1)
     g.affine_select(T.ident[:], T.ones128[:], [[-1, 128]], A.is_equal, 0.0, 0, 1).then_inc(S.si, 1)
     g.vector.wait_ge(S.si, 1)
     g.vector.tensor_copy(T.identb[:], T.ident[:]).then_inc(S.sib, 1)
-    for h in range(2):
+    g.scalar.wait_ge(S.so, 1)
+    g.scalar.activation(T.onesb[:], T.ones128[:], Act.Sqrt).then_inc(S.sob, 1)
+    for h in (1, 0):
         g.scalar.wait_ge(S["sx%d" % h], 16)
         g.scalar.activation(T.x2[:, 256 * h:256 * h + 256], T.xs[:, 256 * h:256 * h + 256], Act.Square).then_inc(S["sq%d" % h], 1)
+    sent = 0
+    g.wait_ge(S.sw, 16)
+    sent += _send(g, core, T, topo, agent[k], T.ws[:], T.WA[:, 128 * i:128 * i + 128], S.aW, _common(core, agent[k], topo))
+    g.wait_ge(S.sx1, 16)
+    trs = []
+    for h in range(2):
+        rid, pid = topo.addr(agent[k][h], core)
+        eng = _raw_engines(core, k, h, agent, topo)
+        trs.append(RemoteDMATransfer(dst_ids=[DstId(rid=rid, pnc=pid)], dma_engine_mask=_mk(eng), remote_sem=S.aR,
+                                     srcs=[T.xs[:, CW * (2 + h):CW * (2 + h) + CW]], dsts=[T.XA[:, CW * i:CW * i + CW]],
+                                     alu_op=0))
+        sent += len(eng)
+    g.remote_dma_fused(trs, local_sem=S.lsem)
     g.tensor.wait_ge(S.sw, 16)
+    g.tensor.wait_ge(S.sx0, 16)
+    for c in range(2):
+        g.tensor.matmul(T["pc%d" % c][:, 0:CW], T.ws[:], T.xs[:, CW * c:CW * c + CW], True, True).then_inc(S["pm%d" % c], 1)
+    g.tensor.wait_ge(S.sm, 1)
+    g.tensor.wait_ge(S.sq0, 1)
+    g.tensor.wait_ge(S.sq1, 1)
     for c in range(4):
-        g.tensor.wait_ge(S["sx%d" % (c // 2)], 16)
-        g.tensor.matmul(T["pc%d" % c][:, 0:128], T.ws[:], T.xs[:, 128 * c:128 * c + 128], True, True).then_inc(S["pm%d" % c], 1)
-    g.tensor.wait_ge(S.sm, 4)
-    for c in range(4):
-        g.tensor.wait_ge(S["sq%d" % (c // 2)], 1)
-        g.tensor.matmul(T.ps0[:, c:c + 1], T.x2[:, 128 * c:128 * c + 128], T.one3[:, 0:1], True, True).then_inc(S.pss, 1)
-    for c in range(4):
-        q = g.vector if c % 2 == 0 else g.scalar
-        q.wait_ge(S["pm%d" % c], 1)
-        for j in range(3):
-            s = HWD * (c % 2) + QW * (c // 2) + SW * j
-            src = T["pc%d" % c][:, STARTS[j]:STARTS[j] + BW]
-            if c % 2 == 0:
-                q.tensor_copy(T.stg[:, s:s + BW], src).then_inc(S["cp%d" % c], 1)
-            else:
-                q.activation(T.stg[:, s:s + BW], src, Act.Copy).then_inc(S["cp%d" % c], 1)
+        g.tensor.matmul(T.ps0[:, c:c + 1], T.x2[:, CW * c:CW * c + CW], T.one3[:, 0:1], True, True).then_inc(S.pss, 1)
+    for c in range(2):
+        g.vector.wait_ge(S["pm%d" % c], 1)
+        g.vector.tensor_copy(T.stg[:, CW * c:CW * c + CW], T["pc%d" % c][:, 0:CW]).then_inc(S["cp%d" % c], 1)
     g.vector.wait_ge(S.pss, 4)
     g.vector.tensor_copy(T.ssr[:], T.ps0[:, 0:4]).then_inc(S.cps, 1)
     partner = ranks_of[k][1 - i]
-    crs = [courier[k][q] for q in sorted(courier[k]) if courier[k][q] != core]
-    em = _common(core, agent[k] + crs + [partner], topo)[0:8]
-    m = _mk(em)
-    sent = 0
-    for c in range(4):
-        h, e = c % 2, c // 2
-        rid, pid = topo.addr(agent[k][h], core)
-        g.wait_ge(S["cp%d" % c], 3)
-        g.remote_dma(T.L[:, HWD * i + QW * e:HWD * i + QW * e + QW], T.stg[:, HWD * h + QW * e:HWD * h + QW * e + QW],
-                     S["aL%d" % e], S.lsem, pid, rid, m)
+    crs = _ss_dests(core, k, courier)
+    for c in range(2):
+        rid, pid = topo.addr(agent[k][c], core)
+        em = _common(core, [agent[k][c]], topo)
+        g.wait_ge(S["cp%d" % c], 1)
+        g.remote_dma(T.L[:, CW * i:CW * i + CW], T.stg[:, CW * c:CW * c + CW], S.aL0, S.lsem, pid, rid, _mk(em))
         sent += len(em)
     g.wait_ge(S.cps, 1)
-    sent += _send(g, core, T, topo, crs, T.ssr[:], T.LS[:, 4 * i:4 * i + 4], S.arrS, em)
+    sent += _send(g, core, T, topo, crs, T.ssr[:], T.LS[:, 4 * i:4 * i + 4], S.arrS, _common(core, crs, topo))
     for q in sorted(courier[k]):
         if courier[k][q] == core:
             o = 1 - i
-            g.vector.wait_ge(S.arrS, len(em))
+            g.vector.wait_ge(S.arrS, len(_common(partner, _ss_dests(partner, k, courier), topo)))
             g.vector.wait_ge(S.cps, 1)
             g.vector.tensor_tensor(T.CS[:], T.ssr[:], T.LS[:, 4 * o:4 * o + 4], A.add).then_inc(S.css, 1)
             g.wait_ge(S.css, 1)
@@ -186,11 +205,13 @@ def _rank(g, core, T, topo, ranks_of, agent, courier, recv, targets, k):
             n += len(near) if b == k else len(far)
         need.append(n)
     rid, pid = topo.addr(partner, core)
+    ex = _common(core, [partner], topo)
+    exin = len(_common(partner, [core], topo))
     for e in range(2):
-        cs = slice(128 * (hown + 2 * e), 128 * (hown + 2 * e) + 128)
+        cs = slice(CW * (hown + 2 * e), CW * (hown + 2 * e) + CW)
         g.wait_ge(S["aY%d" % e], need[e])
-        g.remote_dma(T.Y[:, cs], T.Y[:, cs], S["aX%d" % e], S.lsem, pid, rid, m)
-        sent += len(em)
+        g.remote_dma(T.Y[:, cs], T.Y[:, cs], S["aX%d" % e], S.lsem, pid, rid, _mk(ex))
+        sent += len(ex)
     myq = [q for q in range(len(targets)) if core in targets[q]][0]
     g.vector.wait_ge(S.arrRS, sum(len(_common(courier[kk][myq], targets[myq], topo)) for kk in range(NCH)))
     for c in range(4):
@@ -206,6 +227,7 @@ def _rank(g, core, T, topo, ranks_of, agent, courier, recv, targets, k):
     g.vector.wait_ge(S.sib, 1)
     g.scalar.wait_ge(S.s5, 1)
     g.scalar.wait_ge(S.sib, 1)
+    g.tensor.wait_ge(S.sob, 1)
     for c in range(4):
         cs = slice(128 * c, 128 * c + 128)
         out = T["bc%d" % (c // 2)][:, 128 * (c % 2):128 * (c % 2) + 128]
@@ -222,7 +244,7 @@ def _rank(g, core, T, topo, ranks_of, agent, courier, recv, targets, k):
             if h == hown:
                 g.vector.wait_ge(S["aY%d" % e], need[e])
             else:
-                g.vector.wait_ge(S["aX%d" % e], len(em))
+                g.vector.wait_ge(S["aX%d" % e], exin)
             g.vector.tensor_tensor(T.Yo[:, cs], T.Y[:, cs], T["bc%d" % (c // 2)][:, 128 * (c % 2):128 * (c % 2) + 128],
                                    A.mult).then_inc(S["y%d" % c], 1)
             q.wait_ge(S["y%d" % c], 1)
@@ -232,9 +254,9 @@ def _rank(g, core, T, topo, ranks_of, agent, courier, recv, targets, k):
         g.wait_ge(S["st%d" % c], 16)
 
 
-def _courier(g, core, T, topo, tg, k):
+def _courier(g, core, T, topo, ranks_of, courier, tg, k):
     S = T.sem
-    g.vector.wait_ge(S.arrS, 16)
+    g.vector.wait_ge(S.arrS, sum(len(_common(r, _ss_dests(r, k, courier), topo)) for r in ranks_of[k]))
     g.vector.tensor_tensor(T.CS[:], T.LS[:, 0:4], T.LS[:, 4:8], AluOpType.add).then_inc(S.css, 1)
     g.wait_ge(S.css, 1)
     g.wait_ge(S.lsem, _send(g, core, T, topo, tg, T.CS[:], T.RS[:, 4 * k:4 * k + 4], S.arrRS, _common(core, tg, topo)))
@@ -243,38 +265,51 @@ def _courier(g, core, T, topo, tg, k):
 def _agent(g, core, T, topo, ranks_of, agent, recv, k, h):
     S = T.sem
     A = AluOpType
-    own = slice(SW * k, SW * k + SW)
+    own = slice(SW * k, SW * k + BW)
     eo = k // 3
-    acc = T.pc0[:, 0:SW]
+    oo = STARTS[k % 3]
+    acc = T.pc0[:, 0:BW]
     sent = 0
+    g.tensor.wait_ge(S.aW, sum(len(_common(r, agent[k], topo)) for r in ranks_of[k]))
+    g.tensor.wait_ge(S.aR, sum(len(_raw_engines(r, k, h, agent, topo)) for r in ranks_of[k]))
+    g.tensor.matmul(T.pc1[:, 0:CW], T.WA[:, 0:128], T.XA[:, 0:CW], True, False)
+    g.tensor.matmul(T.pc1[:, 0:CW], T.WA[:, 128:256], T.XA[:, CW:2 * CW], False, True).then_inc(S.pmA, 1)
     for e in range(2):
-        g.vector.wait_ge(S["aL%d" % e], 16)
-        g.vector.tensor_tensor(T.C[:, QW * e:QW * e + QW], T.L[:, QW * e:QW * e + QW],
-                               T.L[:, HWD + QW * e:HWD + QW * e + QW], A.add).then_inc(S["cs%d" % e], 1)
-        if e == eo:
-            g.vector.tensor_tensor(acc, T.L[:, own], T.L[:, HWD + SW * k:HWD + SW * k + SW], A.add).then_inc(S.t, 1)
+        if e == 0:
+            g.vector.wait_ge(S.aL0, sum(len(_common(r, [core], topo)) for r in ranks_of[k]))
+            g.vector.tensor_tensor(T.C[:, 0:CW], T.L[:, 0:CW], T.L[:, CW:2 * CW], A.add).then_inc(S.cs0, 1)
+            if eo == 0:
+                g.vector.tensor_tensor(acc, T.L[:, oo:oo + BW], T.L[:, CW + oo:CW + oo + BW], A.add).then_inc(S.t, 1)
+        else:
+            g.vector.wait_ge(S.pmA, 1)
+            g.vector.tensor_copy(T.C[:, CW:2 * CW], T.pc1[:, 0:CW]).then_inc(S.cs1, 1)
+            if eo == 1:
+                g.vector.tensor_copy(acc, T.pc1[:, oo:oo + BW]).then_inc(S.t, 1)
         g.wait_ge(S["cs%d" % e], 1)
-        trs = []
-        for b, eng in _scatter_plan(k, h, e, agent, topo):
-            rid, pid = topo.addr(agent[b][h], core)
-            trs.append(RemoteDMATransfer(dst_ids=[DstId(rid=rid, pnc=pid)], dma_engine_mask=_mk(eng),
-                                         remote_sem=S["ar%d" % k], srcs=[T.C[:, SW * b:SW * b + SW]], dsts=[T.R[:, own]],
-                                         alu_op=0))
-            sent += len(eng)
-        g.remote_dma_fused(trs, local_sem=S.lsem)
+        for call in _scatter_plan(h, e, agent, topo)[k]:
+            trs = []
+            for b, eng in call:
+                rid, pid = topo.addr(agent[b][h], core)
+                o = CW * e + STARTS[b % 3]
+                trs.append(RemoteDMATransfer(dst_ids=[DstId(rid=rid, pnc=pid)], dma_engine_mask=_mk(eng),
+                                             remote_sem=S["ar%d" % k], srcs=[T.C[:, o:o + BW]], dsts=[T.R[:, own]],
+                                             alu_op=0))
+                sent += len(eng)
+            g.remote_dma_fused(trs, local_sem=S.lsem)
+    plan = _scatter_plan(h, eo, agent, topo)
     src = []
     for kk in range(NCH):
         if kk != k:
-            cnt = [len(eng) for b, eng in _scatter_plan(kk, h, eo, agent, topo) if b == k][0]
-            src.append((-cnt, 0 if topo.same_plane(core, agent[kk][h]) else 1, kk, cnt))
+            n, cnt = [(n, len(eng)) for n, call in enumerate(plan[kk]) for b, eng in call if b == k][0]
+            src.append((n, 0 if topo.same_plane(core, agent[kk][h]) else 1, kk, cnt))
     src.sort()
     for n, (_, _, kk, cnt) in enumerate(src):
         g.vector.wait_ge(S["ar%d" % kk], cnt)
         g.vector.wait_ge(S.t, n + 1)
-        out = T.T3[:] if n == len(src) - 1 else acc
-        g.vector.tensor_tensor(out, acc, T.R[:, SW * kk:SW * kk + SW], A.add).then_inc(S.t, 1)
+        out = T.T3[:, 0:BW] if n == len(src) - 1 else acc
+        g.vector.tensor_tensor(out, acc, T.R[:, SW * kk:SW * kk + BW], A.add).then_inc(S.t, 1)
     lo = 1 if k % 3 == 2 else 0
-    tok = 128 * (h + 2 * eo) + STARTS[k % 3]
+    tok = CW * (h + 2 * eo) + STARTS[k % 3]
     far, near = _last_engines(k, h, agent, recv, topo)
     g.wait_ge(S.t, len(src) + 1)
     sent += _send(g, core, T, topo, [recv[kk][h] for kk in range(NCH) if kk != k], T.T3[:, lo:BW],
@@ -293,4 +328,4 @@ def rank_program(g, core, T, topo):
         else:
             for q in sorted(courier[k]):
                 if courier[k][q] == core:
-                    _courier(g, core, T, topo, targets[q], k)
+                    _courier(g, core, T, topo, ranks_of, courier, targets[q], k)

@@ -31,7 +31,7 @@ SCRATCH = {
     "bc0": ("psum", [128, 512], F), "bc1": ("psum", [128, 512], F),
 }
 SEMAPHORES = ["so", "sob", "sw", "sx0", "sx1", "sm", "sq0", "sq1", "pm0", "pm1", "pss", "cps", "cp0", "cp1",
-              "aW", "aR", "pmA",
+              "aW", "aR", "pmA", "aI",
               "arrS", "arrRS", "css", "aL0", "aY0", "aY1", "aX0", "aX1", "lsem", "st0", "st1", "st2", "st3",
               "si", "cs0", "cs1", "s1", "s2", "s3", "s4", "s5", "sib", "d0", "d1", "d2", "d3", "b0", "b1",
               "y0", "y1", "y2", "y3", "t", "ar0", "ar1", "ar2", "ar3", "ar4", "ar5"]
@@ -136,15 +136,12 @@ def _rank(g, core, T, topo, ranks_of, agent, courier, recv, targets, k):
     A = AluOpType
     i = ranks_of[k].index(core)
     Act = ActivationFunctionType
+    hown = recv[k].index(core)
     g.sync.dma_start(T.ws[:], T.w[:]).then_inc(S.sw, 16)
     g.scalar.dma_start(T.xs[:, 256:512], T.x[:, 256:512]).then_inc(S.sx1, 16)
     g.sync.dma_start(T.xs[:, 0:256], T.x[:, 0:256]).then_inc(S.sx0, 16)
     g.vector.memset(T.ones128[:], 1.0).then_inc(S.so, 1)
     g.vector.memset(T.one3[:], 1.0).then_inc(S.sm, 1)
-    g.wait_ge(S.so, 1)
-    g.affine_select(T.ident[:], T.ones128[:], [[-1, 128]], A.is_equal, 0.0, 0, 1).then_inc(S.si, 1)
-    g.vector.wait_ge(S.si, 1)
-    g.vector.tensor_copy(T.identb[:], T.ident[:]).then_inc(S.sib, 1)
     g.scalar.wait_ge(S.so, 1)
     g.scalar.activation(T.onesb[:], T.ones128[:], Act.Sqrt).then_inc(S.sob, 1)
     for h in (1, 0):
@@ -196,7 +193,6 @@ def _rank(g, core, T, topo, ranks_of, agent, courier, recv, targets, k):
             g.wait_ge(S.css, 1)
             sent += _send(g, core, T, topo, targets[q], T.CS[:], T.RS[:, 4 * k:4 * k + 4], S.arrRS,
                           _common(core, targets[q], topo))
-    hown = recv[k].index(core)
     need = []
     for e in range(2):
         n = 0
@@ -213,6 +209,7 @@ def _rank(g, core, T, topo, ranks_of, agent, courier, recv, targets, k):
         g.remote_dma(T.Y[:, cs], T.Y[:, cs], S["aX%d" % e], S.lsem, pid, rid, _mk(ex))
         sent += len(ex)
     myq = [q for q in range(len(targets)) if core in targets[q]][0]
+    idn = len(_common(agent[k][hown], [core], topo))
     g.vector.wait_ge(S.arrRS, sum(len(_common(courier[kk][myq], targets[myq], topo)) for kk in range(NCH)))
     for c in range(4):
         g.vector.tensor_reduce(T.sst[:, c:c + 1], T.RS[:, c:4 * NCH:4], AxisListType.X, A.add).then_inc(S.s1, 1)
@@ -224,9 +221,9 @@ def _rank(g, core, T, topo, ranks_of, agent, courier, recv, targets, k):
     g.vector.tensor_copy(T.rh[:], T.rs[:]).then_inc(S.s4, 1)
     g.vector.wait_ge(S.s4, 1)
     g.vector.tensor_tensor(T.rl[:], T.rs[:], T.rh[:], A.subtract).then_inc(S.s5, 1)
-    g.vector.wait_ge(S.sib, 1)
+    g.vector.wait_ge(S.aI, idn)
     g.scalar.wait_ge(S.s5, 1)
-    g.scalar.wait_ge(S.sib, 1)
+    g.scalar.wait_ge(S.aI, idn)
     g.tensor.wait_ge(S.sob, 1)
     for c in range(4):
         cs = slice(128 * c, 128 * c + 128)
@@ -270,6 +267,13 @@ def _agent(g, core, T, topo, ranks_of, agent, recv, k, h):
     oo = STARTS[k % 3]
     acc = T.pc0[:, 0:BW]
     sent = 0
+    g.vector.memset(T.ones128[:], 1.0).then_inc(S.so, 1)
+    g.wait_ge(S.so, 1)
+    g.affine_select(T.ident[:], T.ones128[:], [[-1, 128]], A.is_equal, 0.0, 0, 1).then_inc(S.si, 1)
+    g.vector.wait_ge(S.si, 1)
+    g.vector.tensor_copy(T.identb[:], T.ident[:]).then_inc(S.sib, 1)
+    g.wait_ge(S.sib, 1)
+    sent += _send(g, core, T, topo, [recv[k][h]], T.identb[:], T.identb[:], S.aI, _common(core, [recv[k][h]], topo))
     g.tensor.wait_ge(S.aW, sum(len(_common(r, agent[k], topo)) for r in ranks_of[k]))
     g.tensor.wait_ge(S.aR, sum(len(_raw_engines(r, k, h, agent, topo)) for r in ranks_of[k]))
     g.tensor.matmul(T.pc1[:, 0:CW], T.WA[:, 0:128], T.XA[:, 0:CW], True, False)

from concourse.bass import DstId, RemoteDMATransfer
from concourse.mybir import AluOpType, AxisListType, ActivationFunctionType

WORLD = 256
NR = 12
D = 128 * NR
EPS = 0.01
NCH = 6
BW = 43
SW = 44
CW = 128
HWD = NCH * SW
STARTS = (0, 43, 85)
NEAR = 4

F = "float32"
B = "bfloat16"
SCRATCH = {
    "xs": ("sbuf", [128, 512], F), "ws": ("sbuf", [128, 128], F), "x2": ("sbuf", [128, 512], F),
    "one3": ("sbuf", [128, 4], F), "stg": ("sbuf", [128, 2 * CW], F), "Y": ("sbuf", [128, 512], F),
    "Yo": ("sbuf", [128, 512], F),
    "L": ("sbuf", [128, 2 * CW], F), "C": ("sbuf", [128, 2 * CW], F), "R": ("sbuf", [128, HWD], F),
    "WA": ("sbuf", [128, 2 * 128], F), "XA": ("sbuf", [128, 2 * CW], F),
    "T3": ("sbuf", [128, SW], F),
    "sst": ("sbuf", [128, 4], F), "sq": ("sbuf", [128, 4], F), "rs": ("sbuf", [128, 4], F),
    "ones128": ("sbuf", [128, 128], F), "ident": ("sbuf", [128, 128], F),
    "onesb": ("sbuf", [128, 128], B), "identb": ("sbuf", [128, 128], B), "dgh": ("sbuf", [128, 512], B),
    "dgl": ("sbuf", [128, 512], B), "rh": ("sbuf", [128, 4], B), "rl": ("sbuf", [128, 4], F),
    "ssr": ("sbuf", [128, 4], F), "LS": ("sbuf", [128, 8], F), "CS": ("sbuf", [128, 4], F), "RS": ("sbuf", [128, 4 * NCH], F),
    "pc0": ("psum", [128, 512], F), "pc1": ("psum", [128, 512], F), "ps0": ("psum", [128, 512], F),
    "bc0": ("psum", [128, 512], F), "bc1": ("psum", [128, 512], F),
}
SEMAPHORES = ["so", "sob", "sw", "sx0", "sx1", "sm", "sq0", "sq1", "pm0", "pm1", "pss", "cps", "cp0", "cp1",
              "aW", "aR", "pmA", "aI",
              "arrS", "arrRS", "css", "aL0", "aY0", "aY1", "aX0", "aX1", "lsem", "st0", "st1", "st2", "st3",
              "si", "cs0", "cs1", "s1", "s2", "s3", "s4", "s5", "sib", "d0", "d1", "d2", "d3", "b0", "b1",
              "y0", "y1", "y2", "y3", "t", "ar0", "ar1", "ar2", "ar3", "ar4", "ar5"]


def _bits(m):
    return [i for i in range(16) if (m >> i) & 1]


def _mk(lst):
    return sum(1 << i for i in lst)


def _layout(T, topo):
    ranks = list(T.cores)
    key = lambda c: (topo.host(c), topo.chip(c))
    chips = []
    for c in ranks:
        if key(c) not in chips:
            chips.append(key(c))
    dies = sorted(set(topo.die(c) for c in ranks))
    ranks_of = [[c for c in ranks if key(c) == ch] for ch in chips]
    seen, targets = [], []
    for a in range(NCH):
        if a not in seen:
            b = [b for b in range(a + 1, NCH) if b not in seen and topo.same_plane(ranks_of[a][0], ranks_of[b][0])][0]
            seen += [a, b]
            targets.append(ranks_of[a] + ranks_of[b])
    agent, courier, recv = [], [], []
    for k, ch in enumerate(chips):
        helpers = [c for c in range(WORLD) if key(c) == ch and c not in ranks]
        cand = [c for c in helpers if all(topo.may_write(c, r) for r in ranks)]
        row = [[c for c in cand if topo.die(c) == d][0] for d in dies]
        agent.append(row)
        recv.append([[r for r in ranks_of[k] if topo.die(r) == d][0] for d in dies])
        spare = [c for c in helpers if c not in row]
        spare.sort(key=lambda c: sum(1 for r in ranks if topo.may_write(c, r)))
        able = lambda pool, q, used: [c for c in pool if c not in used and c not in targets[q]
                                      and all(topo.may_write(c, r) for r in targets[q])]
        used, cr = [], {}
        for q in sorted(range(len(targets)), key=lambda q: len(able(spare, q, []))):
            a = able(spare, q, used) or able(ranks_of[k], q, used)
            cr[q] = a[0]
            used.append(a[0])
        courier.append(cr)
    return ranks, ranks_of, agent, courier, recv, targets


def _common(core, dests, topo):
    eng = _bits(topo.mask(core, dests[0]))
    for d in dests:
        eng = [e for e in eng if e in _bits(topo.mask(core, d))]
    return eng


def _ss_dests(r, k, courier):
    return [courier[k][q] for q in sorted(courier[k]) if courier[k][q] != r]


def _raw_engines(r, k, h, agent, topo):
    eng = _common(r, agent[k], topo)
    n = len(eng) // 2
    return eng[n * h:n * h + n]


def _send(g, core, T, topo, dests, src, dst_ap, sem, eng):
    ids = []
    for r in dests:
        rid, pid = topo.addr(r, core)
        ids.append(DstId(rid=rid, pnc=pid))
    g.remote_dma_fused([RemoteDMATransfer(dst_ids=ids, dma_engine_mask=_mk(eng), remote_sem=sem, srcs=[src],
                                          dsts=[dst_ap for _ in dests], alu_op=0)], local_sem=T.sem.lsem)
    return len(eng)


def _scatter_plan(h, e, agent, topo):
    plan, thirds = {}, {}
    for k in range(NCH):
        me = agent[k][h]
        others = [b for b in range(3 * e, 3 * e + 3) if b != k]
        eng = _common(me, [agent[b][h] for b in range(NCH) if b != k], topo)
        n = len(eng)
        calls = []
        if len(others) == 3:
            near = [b for b in others if topo.same_plane(me, agent[b][h])] or others
            last = min(near, key=lambda b: (thirds.get(b, 0), b))
            thirds[last] = thirds.get(last, 0) + 1
            others = [b for b in others if b != last]
            calls = [[(last, eng)]]
        plan[k] = [[(others[0], eng[0:n // 2]), (others[1], eng[n // 2:n])]] + calls
    return plan


def _last_engines(k, h, agent, recv, topo):
    far = _common(agent[k][h], [recv[kk][h] for kk in range(NCH) if kk != k], topo)
    near = [e for e in _common(agent[k][h], [recv[k][h]], topo) if e not in far][0:NEAR]
    return far, near


def _rank(g, core, T, topo, ranks_of, agent, courier, recv, targets, k):
    S = T.sem
    A = AluOpType
    i = ranks_of[k].index(core)
    Act = ActivationFunctionType
    hown = recv[k].index(core)
    g.sync.dma_start(T.ws[:], T.w[:]).then_inc(S.sw, 16)
    g.scalar.dma_start(T.xs[:, 256:512], T.x[:, 256:512]).then_inc(S.sx1, 16)
    g.sync.dma_start(T.xs[:, 0:256], T.x[:, 0:256]).then_inc(S.sx0, 16)
    g.vector.memset(T.ones128[:], 1.0).then_inc(S.so, 1)
    g.vector.memset(T.one3[:], 1.0).then_inc(S.sm, 1)
    g.scalar.wait_ge(S.so, 1)
    g.scalar.activation(T.onesb[:], T.ones128[:], Act.Sqrt).then_inc(S.sob, 1)
    for h in (1, 0):
        g.scalar.wait_ge(S["sx%d" % h], 16)
        g.scalar.activation(T.x2[:, 256 * h:256 * h + 256], T.xs[:, 256 * h:256 * h + 256], Act.Square).then_inc(S["sq%d" % h], 1)
    sent = 0
    g.wait_ge(S.sw, 16)
    sent += _send(g, core, T, topo, agent[k], T.ws[:], T.WA[:, 128 * i:128 * i + 128], S.aW, _common(core, agent[k], topo))
    g.wait_ge(S.sx1, 16)
    trs = []
    for h in range(2):
        rid, pid = topo.addr(agent[k][h], core)
        eng = _raw_engines(core, k, h, agent, topo)
        trs.append(RemoteDMATransfer(dst_ids=[DstId(rid=rid, pnc=pid)], dma_engine_mask=_mk(eng), remote_sem=S.aR,
                                     srcs=[T.xs[:, CW * (2 + h):CW * (2 + h) + CW]], dsts=[T.XA[:, CW * i:CW * i + CW]],
                                     alu_op=0))
        sent += len(eng)
    g.remote_dma_fused(trs, local_sem=S.lsem)
    g.tensor.wait_ge(S.sw, 16)
    g.tensor.wait_ge(S.sx0, 16)
    for c in range(2):
        g.tensor.matmul(T["pc%d" % c][:, 0:CW], T.ws[:], T.xs[:, CW * c:CW * c + CW], True, True).then_inc(S["pm%d" % c], 1)
    g.tensor.wait_ge(S.sm, 1)
    g.tensor.wait_ge(S.sq0, 1)
    g.tensor.wait_ge(S.sq1, 1)
    for c in range(4):
        g.tensor.matmul(T.ps0[:, c:c + 1], T.x2[:, CW * c:CW * c + CW], T.one3[:, 0:1], True, True).then_inc(S.pss, 1)
    for c in range(2):
        g.vector.wait_ge(S["pm%d" % c], 1)
        g.vector.tensor_copy(T.stg[:, CW * c:CW * c + CW], T["pc%d" % c][:, 0:CW]).then_inc(S["cp%d" % c], 1)
    g.vector.wait_ge(S.pss, 4)
    g.vector.tensor_copy(T.ssr[:], T.ps0[:, 0:4]).then_inc(S.cps, 1)
    partner = ranks_of[k][1 - i]
    crs = _ss_dests(core, k, courier)
    for c in range(2):
        rid, pid = topo.addr(agent[k][c], core)
        em = _common(core, [agent[k][c]], topo)
        g.wait_ge(S["cp%d" % c], 1)
        g.remote_dma(T.L[:, CW * i:CW * i + CW], T.stg[:, CW * c:CW * c + CW], S.aL0, S.lsem, pid, rid, _mk(em))
        sent += len(em)
    g.wait_ge(S.cps, 1)
    sent += _send(g, core, T, topo, crs, T.ssr[:], T.LS[:, 4 * i:4 * i + 4], S.arrS, _common(core, crs, topo))
    for q in sorted(courier[k]):
        if courier[k][q] == core:
            o = 1 - i
            g.vector.wait_ge(S.arrS, len(_common(partner, _ss_dests(partner, k, courier), topo)))
            g.vector.wait_ge(S.cps, 1)
            g.vector.tensor_tensor(T.CS[:], T.ssr[:], T.LS[:, 4 * o:4 * o + 4], A.add).then_inc(S.css, 1)
            g.wait_ge(S.css, 1)
            sent += _send(g, core, T, topo, targets[q], T.CS[:], T.RS[:, 4 * k:4 * k + 4], S.arrRS,
                          _common(core, targets[q], topo))
    need = []
    for e in range(2):
        n = 0
        for b in range(3 * e, 3 * e + 3):
            far, near = _last_engines(b, hown, agent, recv, topo)
            n += len(near) if b == k else len(far)
        need.append(n)
    rid, pid = topo.addr(partner, core)
    ex = _common(core, [partner], topo)
    exin = len(_common(partner, [core], topo))
    for e in range(2):
        cs = slice(CW * (hown + 2 * e), CW * (hown + 2 * e) + CW)
        g.wait_ge(S["aY%d" % e], need[e])
        g.remote_dma(T.Y[:, cs], T.Y[:, cs], S["aX%d" % e], S.lsem, pid, rid, _mk(ex))
        sent += len(ex)
    myq = [q for q in range(len(targets)) if core in targets[q]][0]
    idn = len(_common(agent[k][hown], [core], topo))
    g.vector.wait_ge(S.arrRS, sum(len(_common(courier[kk][myq], targets[myq], topo)) for kk in range(NCH)))
    for c in range(4):
        g.vector.tensor_reduce(T.sst[:, c:c + 1], T.RS[:, c:4 * NCH:4], AxisListType.X, A.add).then_inc(S.s1, 1)
    g.scalar.wait_ge(S.s1, 4)
    g.scalar.activation(T.sq[:], T.sst[:], Act.Sqrt, bias=EPS, scale=1.0 / D).then_inc(S.s2, 1)
    g.vector.wait_ge(S.s2, 1)
    g.vector.reciprocal(T.rs[:], T.sq[:]).then_inc(S.s3, 1)
    g.vector.wait_ge(S.s3, 1)
    g.vector.tensor_copy(T.rh[:], T.rs[:]).then_inc(S.s4, 1)
    g.vector.wait_ge(S.s4, 1)
    g.vector.tensor_tensor(T.rl[:], T.rs[:], T.rh[:], A.subtract).then_inc(S.s5, 1)
    g.vector.wait_ge(S.aI, idn)
    g.scalar.wait_ge(S.s5, 1)
    g.scalar.wait_ge(S.aI, idn)
    g.tensor.wait_ge(S.sob, 1)
    for c in range(4):
        cs = slice(128 * c, 128 * c + 128)
        out = T["bc%d" % (c // 2)][:, 128 * (c % 2):128 * (c % 2) + 128]
        g.vector.tensor_scalar(T.dgh[:, cs], T.identb[:], T.rh[:, c:c + 1], None, A.mult).then_inc(S["d%d" % c], 1)
        g.scalar.activation(T.dgl[:, cs], T.identb[:], Act.Copy, scale=T.rl[:, c:c + 1]).then_inc(S["d%d" % c], 1)
        g.tensor.wait_ge(S["d%d" % c], 2)
        g.tensor.matmul(out, T.onesb[:], T.dgh[:, cs], True, False)
        g.tensor.matmul(out, T.onesb[:], T.dgl[:, cs], False, True).then_inc(S["b%d" % (c // 2)], 1)
    for e in range(2):
        for h, q in ((hown, g.sync), (1 - hown, g.scalar)):
            c = h + 2 * e
            cs = slice(128 * c, 128 * c + 128)
            g.vector.wait_ge(S["b%d" % (c // 2)], 2)
            if h == hown:
                g.vector.wait_ge(S["aY%d" % e], need[e])
            else:
                g.vector.wait_ge(S["aX%d" % e], exin)
            g.vector.tensor_tensor(T.Yo[:, cs], T.Y[:, cs], T["bc%d" % (c // 2)][:, 128 * (c % 2):128 * (c % 2) + 128],
                                   A.mult).then_inc(S["y%d" % c], 1)
            q.wait_ge(S["y%d" % c], 1)
            q.dma_start(T.y[:, cs], T.Yo[:, cs]).then_inc(S["st%d" % c], 16)
    g.wait_ge(S.lsem, sent)
    for c in range(4):
        g.wait_ge(S["st%d" % c], 16)


def _courier(g, core, T, topo, ranks_of, courier, tg, k):
    S = T.sem
    g.vector.wait_ge(S.arrS, sum(len(_common(r, _ss_dests(r, k, courier), topo)) for r in ranks_of[k]))
    g.vector.tensor_tensor(T.CS[:], T.LS[:, 0:4], T.LS[:, 4:8], AluOpType.add).then_inc(S.css, 1)
    g.wait_ge(S.css, 1)
    g.wait_ge(S.lsem, _send(g, core, T, topo, tg, T.CS[:], T.RS[:, 4 * k:4 * k + 4], S.arrRS, _common(core, tg, topo)))


def _agent(g, core, T, topo, ranks_of, agent, recv, k, h):
    S = T.sem
    A = AluOpType
    own = slice(SW * k, SW * k + BW)
    eo = k // 3
    oo = STARTS[k % 3]
    acc = T.pc0[:, 0:BW]
    sent = 0
    g.vector.memset(T.ones128[:], 1.0).then_inc(S.so, 1)
    g.wait_ge(S.so, 1)
    g.affine_select(T.ident[:], T.ones128[:], [[-1, 128]], A.is_equal, 0.0, 0, 1).then_inc(S.si, 1)
    g.vector.wait_ge(S.si, 1)
    g.vector.tensor_copy(T.identb[:], T.ident[:]).then_inc(S.sib, 1)
    g.wait_ge(S.sib, 1)
    sent += _send(g, core, T, topo, [recv[k][h]], T.identb[:], T.identb[:], S.aI, _common(core, [recv[k][h]], topo))
    g.tensor.wait_ge(S.aW, sum(len(_common(r, agent[k], topo)) for r in ranks_of[k]))
    g.tensor.wait_ge(S.aR, sum(len(_raw_engines(r, k, h, agent, topo)) for r in ranks_of[k]))
    g.tensor.matmul(T.pc1[:, 0:CW], T.WA[:, 0:128], T.XA[:, 0:CW], True, False)
    g.tensor.matmul(T.pc1[:, 0:CW], T.WA[:, 128:256], T.XA[:, CW:2 * CW], False, True).then_inc(S.pmA, 1)
    for e in range(2):
        if e == 0:
            g.vector.wait_ge(S.aL0, sum(len(_common(r, [core], topo)) for r in ranks_of[k]))
            g.vector.tensor_tensor(T.C[:, 0:CW], T.L[:, 0:CW], T.L[:, CW:2 * CW], A.add).then_inc(S.cs0, 1)
            if eo == 0:
                g.vector.tensor_tensor(acc, T.L[:, oo:oo + BW], T.L[:, CW + oo:CW + oo + BW], A.add).then_inc(S.t, 1)
        else:
            g.vector.wait_ge(S.pmA, 1)
            g.vector.tensor_copy(T.C[:, CW:2 * CW], T.pc1[:, 0:CW]).then_inc(S.cs1, 1)
            if eo == 1:
                g.vector.tensor_copy(acc, T.pc1[:, oo:oo + BW]).then_inc(S.t, 1)
        g.wait_ge(S["cs%d" % e], 1)
        for call in _scatter_plan(h, e, agent, topo)[k]:
            trs = []
            for b, eng in call:
                rid, pid = topo.addr(agent[b][h], core)
                o = CW * e + STARTS[b % 3]
                trs.append(RemoteDMATransfer(dst_ids=[DstId(rid=rid, pnc=pid)], dma_engine_mask=_mk(eng),
                                             remote_sem=S["ar%d" % k], srcs=[T.C[:, o:o + BW]], dsts=[T.R[:, own]],
                                             alu_op=0))
                sent += len(eng)
            g.remote_dma_fused(trs, local_sem=S.lsem)
    plan = _scatter_plan(h, eo, agent, topo)
    src = []
    for kk in range(NCH):
        if kk != k:
            n, cnt = [(n, len(eng)) for n, call in enumerate(plan[kk]) for b, eng in call if b == k][0]
            src.append((n, 0 if topo.same_plane(core, agent[kk][h]) else 1, kk, cnt))
    src.sort()
    for n, (_, _, kk, cnt) in enumerate(src):
        g.vector.wait_ge(S["ar%d" % kk], cnt)
        g.vector.wait_ge(S.t, n + 1)
        out = T.T3[:, 0:BW] if n == len(src) - 1 else acc
        g.vector.tensor_tensor(out, acc, T.R[:, SW * kk:SW * kk + BW], A.add).then_inc(S.t, 1)
    lo = 1 if k % 3 == 2 else 0
    tok = CW * (h + 2 * eo) + STARTS[k % 3]
    far, near = _last_engines(k, h, agent, recv, topo)
    g.wait_ge(S.t, len(src) + 1)
    sent += _send(g, core, T, topo, [recv[kk][h] for kk in range(NCH) if kk != k], T.T3[:, lo:BW],
                  T.Y[:, tok + lo:tok + BW], S["aY%d" % eo], far)
    sent += _send(g, core, T, topo, [recv[k][h]], T.T3[:, lo:BW], T.Y[:, tok + lo:tok + BW], S["aY%d" % eo], near)
    g.wait_ge(S.lsem, sent)


def rank_program(g, core, T, topo):
    ranks, ranks_of, agent, courier, recv, targets = _layout(T, topo)
    for k in range(NCH):
        if core in ranks_of[k]:
            _rank(g, core, T, topo, ranks_of, agent, courier, recv, targets, k)
        elif core in agent[k]:
            _agent(g, core, T, topo, ranks_of, agent, recv, k, agent[k].index(core))
        else:
            for q in sorted(courier[k]):
                if courier[k][q] == core:
                    _courier(g, core, T, topo, ranks_of, courier, targets[q], k)
